import numpy as np
import ml_dtypes


def mxq(x, axis, fmt="e4m3"):
    dtype, down = {"e4m3": (ml_dtypes.float8_e4m3fn, 7), "e5m2": (ml_dtypes.float8_e5m2, 14)}[fmt]
    v = np.moveaxis(np.asarray(x, np.float32).astype(ml_dtypes.bfloat16).astype(np.float64), axis, -1)
    blocks = v.reshape(v.shape[:-1] + (-1, 32))
    amax = np.abs(blocks).max(-1, keepdims=True)
    byte = np.maximum(np.where(amax > 0, np.frexp(amax)[1] - 1 + 127, 0) - down, 1)
    scale = np.exp2(byte - 127.0)
    codes = (blocks / scale).astype(np.float32).astype(dtype).astype(np.float64)
    return np.moveaxis((codes * scale).reshape(v.shape), -1, axis)


WIDE = False


def mx_kscale(k):
    if not WIDE:
        return np.ones(k)
    levels = np.array([10, -10, 5, -5, 0])
    if k % 512:
        return np.exp2(np.random.permutation(np.resize(levels, k // 32))).repeat(32)
    a = np.empty((k // 512, 16))
    for p in range(k // 512):
        a[p, :8] = np.random.permutation(np.resize(levels, 8))
        for g in range(8):
            far = levels[np.abs(levels - a[p, g]) >= 10]
            a[p, g + 8] = far[np.random.randint(len(far))]
    return np.exp2(a.ravel()).repeat(32)


def f64(x):
    return np.asarray(x).astype(np.float64)


def striped8(idx):
    return np.concatenate([v.reshape(-1, 16).T for v in idx]).astype(np.uint16)


def unstriped8(offs):
    return np.stack([offs[16 * g:16 * g + 16].T.reshape(-1) for g in range(8)]).astype(np.int64)


E2M1 = np.array([0.0, 0.5, 1.0, 1.5, 2.0, 3.0, 4.0, 6.0, -0.0, -0.5, -1.0, -1.5, -2.0, -3.0, -4.0, -6.0])


def pack_weight(w, fmt):
    k, n = w.shape
    w = f64(np.asarray(w, np.float32).astype(ml_dtypes.bfloat16)).reshape(k // 32, 32, n)
    amax = np.abs(w).max(1)
    if fmt == "e4m3":
        byte = np.frexp(amax)[1] - 1 + 127 - 7
    else:
        mant, ex = np.frexp(amax / 6.0)
        byte = np.where(mant > 0.5, ex, ex - 1) + 127
    byte = np.clip(np.where(amax > 0, byte, 1), 1, 254)
    scaled = (w * np.exp2(127.0 - byte)[:, None, :]).reshape(k, n).astype(np.float32)
    by_word = np.ascontiguousarray(scaled.reshape(k // 512, 128, 4, n).transpose(0, 1, 3, 2))
    if fmt == "e4m3":
        words = by_word.astype(ml_dtypes.float8_e4m3fn).view(np.uint8)
    else:
        c = by_word.astype(ml_dtypes.float4_e2m1fn).view(np.uint8) & 0xF
        words = (c[..., 0::2] | (c[..., 1::2] << 4)).reshape(k // 512, 128, 2 * n)
    return np.ascontiguousarray(words), np.ascontiguousarray(byte.astype(np.uint8).reshape(k // 512, 16, n))


def unpack_weight(words, scales, fmt):
    g, _, n = scales.shape
    words = np.ascontiguousarray(words).reshape(g, 128, n, -1)
    if fmt == "e4m3":
        vals = words.view(ml_dtypes.float8_e4m3fn).astype(np.float64)
    else:
        nib = np.empty((g, 128, n, 4), np.uint8)
        nib[..., 0::2] = words & 0xF
        nib[..., 1::2] = words >> 4
        vals = E2M1[nib]
    vals = vals * np.repeat(np.exp2(scales.astype(np.float64) - 127.0), 8, axis=1)[..., None]
    return vals.transpose(0, 1, 3, 2).reshape(g * 512, n)


def silu(v):
    return v / (1.0 + np.exp(-np.maximum(v, -700.0)))


K, L, M, T, S = 512, 512, 512, 2048, 1024


def setup_inputs():
    n = np.random.standard_normal
    s1 = mx_kscale(K)[:, None]
    s2 = mx_kscale(L)[:, None]
    p_w4 = pack_weight(n((K, M)) / np.sqrt(K) / s1, "e2m1")
    return {
        "xT": (n((K, T)) * s1).astype(np.float32),
        "w4_words": p_w4[0],
        "w4_scales": p_w4[1],
        "c": (n((L, S)) * s2).astype(np.float32),
        "u": (n((L, M)) / np.sqrt(L) / s2).astype(np.float32),
        "wgt": np.repeat(np.random.uniform(0.5, 2.0, (8, S)), 16, axis=0).astype(np.float32),
        "b": (0.3 * n(512)).astype(np.float32),
        "offs": striped8(np.stack([np.random.permutation(T)[:S] for _ in range(8)])),
    }


def reference(xT, w4_words, w4_scales, c, u, wgt, b, offs):
    idx = unstriped8(offs)
    group = np.arange(K) % 512 // 64
    xg = f64(wgt)[np.arange(K) // 4 % 128] * f64(xT)[np.arange(K)[:, None], idx[group]]
    xT_ = mxq(xg, 0, "e4m3")
    w4_ = unpack_weight(w4_words, w4_scales, "e2m1")
    c_ = mxq(f64(c), 0, "e4m3")
    u_ = mxq(f64(u), 0, "e4m3")
    y = w4_.T @ xT_ + u_.T @ c_
    return silu(y + f64(b)[:, None])

@@ -1,0 +1,170 @@
+from contextlib import ExitStack
+
+import concourse.mybir as mybir
+
+K, L, M, T, S = 512, 512, 512, 2048, 1024
+FLOPS = 2 * (K + L) * M * S
+
+F32 = mybir.dt.float32
+BF16 = mybir.dt.bfloat16
+I32 = mybir.dt.int32
+U32 = mybir.dt.uint32
+U16 = mybir.dt.uint16
+U8 = mybir.dt.uint8
+FP8X4 = mybir.dt.float8_e4m3fn_x4
+FP4X4 = mybir.dt.float4_e2m1fn_x4
+MULT = mybir.AluOpType.mult
+SILU = mybir.ActivationFunctionType.Silu
+
+P = 128
+PACK = 4
+HALF = 512
+N_PASS = 128
+CHUNKS = [256, 256, 256, 256]
+C_ON_VECTOR = [False, False, True, True]
+U_ON_VECTOR = [False, True]
+P23_ON_VECTOR = [True, True, True, True]
+
+
+def tile_list_hmix_silu_kernel(tc, xT, w4_words, w4_scales, c, u, wgt, b, offs, out):
+    nc = tc.nc
+    starts = [sum(CHUNKS[:i]) for i in range(len(CHUNKS))]
+
+    def interleave(on_vector, dst, src):
+        d = dst.rearrange("p (g e) i -> p g i e", e=4)
+        s = src.rearrange("p i (g e) -> p g i e", e=4)
+        if on_vector:
+            nc.vector.tensor_copy(out=d, in_=s)
+        else:
+            nc.scalar.copy(out=d, in_=s)
+
+    def interleave_pair(on_vector, dst, src):
+        s = src.rearrange("p i j -> p j i")
+        if on_vector:
+            nc.vector.tensor_copy(out=dst, in_=s)
+        else:
+            nc.scalar.copy(out=dst, in_=s)
+
+    def quantize(codes, scales, grouped):
+        nc.vector.quantize_mx(out=codes.bitcast(FP8X4), scales=scales, in_=grouped.rearrange("p j i -> p (j i)"))
+
+    with ExitStack() as ctx:
+        keep = ctx.enter_context(tc.tile_pool(name="keep", bufs=1))
+        psum = ctx.enter_context(tc.psum_pool(name="psum", bufs=1))
+
+        offsets = keep.tile([P, S // 16], U16, name="offsets")
+        nc.sync.dma_start(offsets[:], offs)
+
+        warm_in = keep.tile([P, 8], F32, name="warm_in")
+        warm_out = keep.tile([P, 8], F32, name="warm_out")
+        nc.vector.memset(warm_in[:], 0.0)
+        nc.scalar.activation(out=warm_out[:], in_=warm_in[:], func=SILU)
+
+        w4_plane = keep.tile([P, M], U8, name="w4_plane", align_bytes=64)
+        nc.vector.memset(w4_plane[:].bitcast(I32), 0)
+        for q in range(4):
+            nc.gpsimd.dma_start(w4_plane[32 * q : 32 * q + 4, :].bitcast(I32), w4_scales[0][4 * q : 4 * q + 4, :].bitcast(I32))
+        bias = keep.tile([P, M // P], F32, name="bias")
+        with nc.allow_non_contiguous_dma(reason="one bias value for each output row"):
+            nc.gpsimd.dma_start(bias[:], b.rearrange("(t p) -> p t", p=P))
+
+        x_rows = xT.rearrange("(p i) t -> p i t", i=PACK)
+        c_rows = c.rearrange("(p i) j -> p i j", i=PACK)
+        u_rows = u.rearrange("(p i) n -> p i n", i=PACK)
+        out_rows = out.rearrange("(t p) j -> p t j", p=P)
+
+        weights = [keep.tile([P, HALF], F32, name=f"weights{h}") for h in range(2)]
+        planes = [keep.tile([P, T], F32, name=f"plane{i}") for i in range(PACK)]
+        w4_codes = keep.tile([P, 2 * M], U8, name="w4_codes", align_bytes=64)
+        u_raw = [keep.tile([P, PACK, 256], F32, name=f"u_raw{h}") for h in range(2)]
+        c_raw = [keep.tile([P, PACK, w], F32, name=f"c_raw{n}") for n, w in enumerate(CHUNKS)]
+
+        nc.sync.dma_start(weights[0][:], wgt[:, 0:HALF])
+        nc.sync.dma_start(planes[0][:], x_rows[:, 0, :])
+        nc.sync.dma_start(weights[1][:], wgt[:, HALF:S])
+        for i in range(1, PACK):
+            nc.sync.dma_start(planes[i][:], x_rows[:, i, :])
+        nc.sync.dma_start(w4_codes[:].bitcast(I32), w4_words[0].bitcast(I32))
+        nc.sync.dma_start(u_raw[0][:], u_rows[:, :, 0:256])
+        nc.sync.dma_start(c_raw[0][:], c_rows[:, :, 0 : CHUNKS[0]])
+        nc.sync.dma_start(u_raw[1][:], u_rows[:, :, 256:512])
+        for n in range(1, len(CHUNKS)):
+            nc.sync.dma_start(c_raw[n][:], c_rows[:, :, starts[n] : starts[n] + CHUNKS[n]])
+
+        picked = [[keep.tile([P, 2, HALF], F32, name=f"picked{pair}_{h}") for h in range(2)] for pair in range(2)]
+
+        def gather(i, j0, width):
+            h, a = divmod(j0, HALF)
+            nc.vector.tensor_tensor(
+                picked[i // 2][h][:, i % 2, a : a + width],
+                planes[i][:].indirect(offsets[:, j0 // 16 : (j0 + width) // 16]),
+                weights[h][:, a : a + width],
+                MULT,
+            )
+
+        x_grouped = [keep.tile([P, w, PACK], BF16, name=f"x_grouped{n}", align_bytes=64) for n, w in enumerate(CHUNKS)]
+        c_grouped = [keep.tile([P, w, PACK], BF16, name=f"c_grouped{n}", align_bytes=64) for n, w in enumerate(CHUNKS)]
+        u_grouped = [keep.tile([P, 256, PACK], BF16, name=f"u_grouped{h}", align_bytes=64) for h in range(2)]
+        x_codes = [keep.tile([P, w], U32, name=f"x_codes{n}", align_bytes=64) for n, w in enumerate(CHUNKS)]
+        c_codes = [keep.tile([P, w], U32, name=f"c_codes{n}", align_bytes=64) for n, w in enumerate(CHUNKS)]
+        u_codes = [keep.tile([P, 256], U32, name=f"u_codes{h}", align_bytes=64) for h in range(2)]
+        x_scales = [keep.tile([P, w], U8, name=f"x_scales{n}", align_bytes=64) for n, w in enumerate(CHUNKS)]
+        c_scales = [keep.tile([P, w], U8, name=f"c_scales{n}", align_bytes=64) for n, w in enumerate(CHUNKS)]
+        u_scales = [keep.tile([P, 256], U8, name=f"u_scales{h}", align_bytes=64) for h in range(2)]
+
+        def pair_to_grouped(pair, n, on_vector):
+            h, a = divmod(starts[n], HALF)
+            interleave_pair(on_vector, x_grouped[n][:, :, 2 * pair : 2 * pair + 2], picked[pair][h][:, :, a : a + CHUNKS[n]])
+
+        def multiply(n, h):
+            w = CHUNKS[n]
+            acc = psum.tile([P, 2, w], F32, name=f"acc{n}_{h}")
+            res = keep.tile([P, 2, w], F32, name=f"res{n}_{h}")
+            for s in range(2):
+                t = 2 * h + s
+                for a in range(0, w, N_PASS):
+                    cols = slice(a, a + N_PASS)
+                    nc.tensor.matmul_mx(
+                        out=acc[:, s, cols],
+                        lhsT=w4_codes[:, 2 * P * t : 2 * P * (t + 1)].bitcast(FP4X4),
+                        lhsT_scale=w4_plane[:, P * t : P * (t + 1)],
+                        rhs=x_codes[n][:, cols].bitcast(FP8X4),
+                        rhs_scale=x_scales[n][:, cols],
+                        start=True,
+                        stop=False,
+                    )
+                    nc.tensor.matmul_mx(
+                        out=acc[:, s, cols],
+                        lhsT=u_codes[h][:, P * s : P * (s + 1)].bitcast(FP8X4),
+                        lhsT_scale=u_scales[h][:, P * s : P * (s + 1)],
+                        rhs=c_codes[n][:, cols].bitcast(FP8X4),
+                        rhs_scale=c_scales[n][:, cols],
+                        start=False,
+                        stop=True,
+                    )
+            for s in range(2):
+                t = 2 * h + s
+                nc.scalar.activation(out=res[:, s, :], in_=acc[:, s, :], func=SILU, bias=bias[:, t : t + 1])
+            nc.sync.dma_start(out_rows[:, 2 * h : 2 * h + 2, starts[n] : starts[n] + w], res[:])
+
+        for i in range(3):
+            for h in range(2):
+                gather(i, h * HALF, HALF)
+            if i == 1:
+                for n in range(len(CHUNKS)):
+                    pair_to_grouped(0, n, False)
+
+        for n, w in enumerate(CHUNKS):
+            gather(3, starts[n], w)
+            pair_to_grouped(1, n, P23_ON_VECTOR[n])
+            if n == 0:
+                interleave(U_ON_VECTOR[0], u_grouped[0][:], u_raw[0][:])
+                quantize(u_codes[0][:], u_scales[0][:], u_grouped[0][:])
+            interleave(C_ON_VECTOR[n], c_grouped[n][:], c_raw[n][:])
+            quantize(x_codes[n][:], x_scales[n][:], x_grouped[n][:])
+            quantize(c_codes[n][:], c_scales[n][:], c_grouped[n][:])
+            multiply(n, 0)
+            if n == 0:
+                interleave(U_ON_VECTOR[1], u_grouped[1][:], u_raw[1][:])
+                quantize(u_codes[1][:], u_scales[1][:], u_grouped[1][:])
+            multiply(n, 1)

@@ -1,6 +1,7 @@
 from contextlib import ExitStack
 
 import concourse.mybir as mybir
+from concourse.masks import make_identity
 
 K, L, M, T, S = 512, 512, 512, 2048, 1024
 FLOPS = 2 * (K + L) * M * S
@@ -17,42 +18,33 @@ MULT = mybir.AluOpType.mult
 SILU = mybir.ActivationFunctionType.Silu
 
 P = 128
-PACK = 4
-HALF = 512
-N_PASS = 128
-CHUNKS = [256, 256, 256, 256]
-C_ON_VECTOR = [False, False, True, True]
-U_ON_VECTOR = [False, True]
-P23_ON_VECTOR = [True, True, True, True]
+PLANES = 4
+LIST_GROUP = 16
+QUADRANT = 32
+ROW_TILES = M // P
+CHUNK = 256
+CHUNKS = S // CHUNK
+W4_PASS = 128
+BANK_TILES = 2
+BANKS = 8
 
 
 def tile_list_hmix_silu_kernel(tc, xT, w4_words, w4_scales, c, u, wgt, b, offs, out):
     nc = tc.nc
-    starts = [sum(CHUNKS[:i]) for i in range(len(CHUNKS))]
+    on_vector, on_scalar = nc.vector.tensor_copy, nc.scalar.copy
+    chunk = [slice(n * CHUNK, (n + 1) * CHUNK) for n in range(CHUNKS)]
+    halves = [slice(0, S // 2), slice(S // 2, S)]
 
-    def interleave(on_vector, dst, src):
-        d = dst.rearrange("p (g e) i -> p g i e", e=4)
-        s = src.rearrange("p i (g e) -> p g i e", e=4)
-        if on_vector:
-            nc.vector.tensor_copy(out=d, in_=s)
-        else:
-            nc.scalar.copy(out=d, in_=s)
-
-    def interleave_pair(on_vector, dst, src):
-        s = src.rearrange("p i j -> p j i")
-        if on_vector:
-            nc.vector.tensor_copy(out=dst, in_=s)
-        else:
-            nc.scalar.copy(out=dst, in_=s)
-
-    def quantize(codes, scales, grouped):
-        nc.vector.quantize_mx(out=codes.bitcast(FP8X4), scales=scales, in_=grouped.rearrange("p j i -> p (j i)"))
+    x_rows = xT.rearrange("(p i) t -> p i t", i=PLANES)
+    c_rows = c.rearrange("(p i) j -> p i j", i=PLANES)
+    u_rows = u.rearrange("(p i) n -> p i n", i=PLANES)
+    out_rows = out.rearrange("(t p) j -> p t j", p=P)
 
     with ExitStack() as ctx:
         keep = ctx.enter_context(tc.tile_pool(name="keep", bufs=1))
-        psum = ctx.enter_context(tc.psum_pool(name="psum", bufs=1))
+        psum = ctx.enter_context(tc.psum_pool(name="psum", bufs=BANKS))
 
-        offsets = keep.tile([P, S // 16], U16, name="offsets")
+        offsets = keep.tile([P, S // LIST_GROUP], U16, name="offsets")
         nc.sync.dma_start(offsets[:], offs)
 
         warm_in = keep.tile([P, 8], F32, name="warm_in")
@@ -60,111 +52,158 @@ def tile_list_hmix_silu_kernel(tc, xT, w4_words, w4_scales, c, u, wgt, b, offs, 
         nc.vector.memset(warm_in[:], 0.0)
         nc.scalar.activation(out=warm_out[:], in_=warm_in[:], func=SILU)
 
+        identity = keep.tile([P, P], F32, name="identity")
+        make_identity(nc, identity[:])
+        bias_rows = keep.tile([P, P], F32, name="bias_rows")
+        nc.vector.memset(bias_rows[:], 0.0)
         w4_plane = keep.tile([P, M], U8, name="w4_plane", align_bytes=64)
         nc.vector.memset(w4_plane[:].bitcast(I32), 0)
-        for q in range(4):
-            nc.gpsimd.dma_start(w4_plane[32 * q : 32 * q + 4, :].bitcast(I32), w4_scales[0][4 * q : 4 * q + 4, :].bitcast(I32))
-        bias = keep.tile([P, M // P], F32, name="bias")
-        with nc.allow_non_contiguous_dma(reason="one bias value for each output row"):
-            nc.gpsimd.dma_start(bias[:], b.rearrange("(t p) -> p t", p=P))
 
-        x_rows = xT.rearrange("(p i) t -> p i t", i=PACK)
-        c_rows = c.rearrange("(p i) j -> p i j", i=PACK)
-        u_rows = u.rearrange("(p i) n -> p i n", i=PACK)
-        out_rows = out.rearrange("(t p) j -> p t j", p=P)
-
-        weights = [keep.tile([P, HALF], F32, name=f"weights{h}") for h in range(2)]
-        planes = [keep.tile([P, T], F32, name=f"plane{i}") for i in range(PACK)]
+        weights = keep.tile([P, S], F32, name="weights")
+        windows = [keep.tile([P, T], F32, name=f"window{i}") for i in range(PLANES)]
         w4_codes = keep.tile([P, 2 * M], U8, name="w4_codes", align_bytes=64)
-        u_raw = [keep.tile([P, PACK, 256], F32, name=f"u_raw{h}") for h in range(2)]
-        c_raw = [keep.tile([P, PACK, w], F32, name=f"c_raw{n}") for n, w in enumerate(CHUNKS)]
 
-        nc.sync.dma_start(weights[0][:], wgt[:, 0:HALF])
-        nc.sync.dma_start(planes[0][:], x_rows[:, 0, :])
-        nc.sync.dma_start(weights[1][:], wgt[:, HALF:S])
-        for i in range(1, PACK):
-            nc.sync.dma_start(planes[i][:], x_rows[:, i, :])
+        first_pair = keep.tile([P, 2, S], F32, name="first_pair")
+        stage = keep.tile([P, 1 + PLANES, S], F32, name="stage")
+        picked = [first_pair[:], stage[:, 0:2, :]]
+        own = [keep.tile([P, PLANES, CHUNK], F32, name=f"raw{r}") for r in range(CHUNKS)]
+        c_raw = [stage[:, 1:, chunk[2]]] + [r[:] for r in own[1:]]
+        u_raw = [stage[:, 1:, chunk[3]], own[0][:]]
+
+        widths = {"x": S, "c": S, "u": M}
+        grouped = {v: keep.tile([P, w, PLANES], BF16, name=f"{v}_grouped", align_bytes=64) for v, w in widths.items()}
+        codes = {v: keep.tile([P, w], U32, name=f"{v}_codes", align_bytes=64) for v, w in widths.items()}
+        scales = {v: keep.tile([P, w], U8, name=f"{v}_scales", align_bytes=64) for v, w in widths.items()}
+
+        nc.sync.dma_start(weights[:, halves[0]], wgt[:, halves[0]])
+        nc.sync.dma_start(windows[0][:], x_rows[:, 0, :])
+        nc.sync.dma_start(weights[:, halves[1]], wgt[:, halves[1]])
+        nc.sync.dma_start(windows[1][:], x_rows[:, 1, :])
+        nc.sync.dma_start(windows[2][:], x_rows[:, 2, :])
+        nc.scalar.dma_start(bias_rows[0:ROW_TILES, :], b.rearrange("(t p) -> t p", p=P))
+        for q in range(P // QUADRANT):
+            nc.scalar.dma_start(
+                w4_plane[QUADRANT * q : QUADRANT * q + 4, :].bitcast(I32),
+                w4_scales[0][4 * q : 4 * q + 4, :].bitcast(I32),
+            )
+        nc.sync.dma_start(windows[3][:], x_rows[:, 3, :])
         nc.sync.dma_start(w4_codes[:].bitcast(I32), w4_words[0].bitcast(I32))
-        nc.sync.dma_start(u_raw[0][:], u_rows[:, :, 0:256])
-        nc.sync.dma_start(c_raw[0][:], c_rows[:, :, 0 : CHUNKS[0]])
-        nc.sync.dma_start(u_raw[1][:], u_rows[:, :, 256:512])
-        for n in range(1, len(CHUNKS)):
-            nc.sync.dma_start(c_raw[n][:], c_rows[:, :, starts[n] : starts[n] + CHUNKS[n]])
+        nc.sync.dma_start(c_raw[0], c_rows[:, :, chunk[0]])
+        for h in range(2):
+            nc.sync.dma_start(u_raw[h], u_rows[:, :, chunk[h]])
+        for n in range(1, CHUNKS):
+            nc.sync.dma_start(c_raw[n], c_rows[:, :, chunk[n]])
 
-        picked = [[keep.tile([P, 2, HALF], F32, name=f"picked{pair}_{h}") for h in range(2)] for pair in range(2)]
+        bias_bank = psum.tile([P, P], F32, name="bank")
+        nc.tensor.transpose(bias_bank[:], bias_rows[:], identity[:])
+        bias = keep.tile([P, ROW_TILES], F32, name="bias")
+        nc.scalar.copy(out=bias[:], in_=bias_bank[:, 0:ROW_TILES])
 
-        def gather(i, j0, width):
-            h, a = divmod(j0, HALF)
+        def gather(i, places):
             nc.vector.tensor_tensor(
-                picked[i // 2][h][:, i % 2, a : a + width],
-                planes[i][:].indirect(offsets[:, j0 // 16 : (j0 + width) // 16]),
-                weights[h][:, a : a + width],
+                picked[i // 2][:, i % 2, places],
+                windows[i][:].indirect(offsets[:, places.start // LIST_GROUP : places.stop // LIST_GROUP]),
+                weights[:, places],
                 MULT,
             )
 
-        x_grouped = [keep.tile([P, w, PACK], BF16, name=f"x_grouped{n}", align_bytes=64) for n, w in enumerate(CHUNKS)]
-        c_grouped = [keep.tile([P, w, PACK], BF16, name=f"c_grouped{n}", align_bytes=64) for n, w in enumerate(CHUNKS)]
-        u_grouped = [keep.tile([P, 256, PACK], BF16, name=f"u_grouped{h}", align_bytes=64) for h in range(2)]
-        x_codes = [keep.tile([P, w], U32, name=f"x_codes{n}", align_bytes=64) for n, w in enumerate(CHUNKS)]
-        c_codes = [keep.tile([P, w], U32, name=f"c_codes{n}", align_bytes=64) for n, w in enumerate(CHUNKS)]
-        u_codes = [keep.tile([P, 256], U32, name=f"u_codes{h}", align_bytes=64) for h in range(2)]
-        x_scales = [keep.tile([P, w], U8, name=f"x_scales{n}", align_bytes=64) for n, w in enumerate(CHUNKS)]
-        c_scales = [keep.tile([P, w], U8, name=f"c_scales{n}", align_bytes=64) for n, w in enumerate(CHUNKS)]
-        u_scales = [keep.tile([P, 256], U8, name=f"u_scales{h}", align_bytes=64) for h in range(2)]
+        def group_pair(copy, h, places):
+            copy(out=grouped["x"][:, places, 2 * h : 2 * h + 2], in_=picked[h][:, :, places].rearrange("p i j -> p j i"))
 
-        def pair_to_grouped(pair, n, on_vector):
-            h, a = divmod(starts[n], HALF)
-            interleave_pair(on_vector, x_grouped[n][:, :, 2 * pair : 2 * pair + 2], picked[pair][h][:, :, a : a + CHUNKS[n]])
+        def group(copy, name, raw, columns):
+            copy(
+                out=grouped[name][:, columns, :].rearrange("p (g e) i -> p g i e", e=4),
+                in_=raw.rearrange("p i (g e) -> p g i e", e=4),
+            )
 
-        def multiply(n, h):
-            w = CHUNKS[n]
-            acc = psum.tile([P, 2, w], F32, name=f"acc{n}_{h}")
-            res = keep.tile([P, 2, w], F32, name=f"res{n}_{h}")
-            for s in range(2):
-                t = 2 * h + s
-                for a in range(0, w, N_PASS):
-                    cols = slice(a, a + N_PASS)
+        def quantize(name, columns):
+            nc.vector.quantize_mx(
+                out=codes[name][:, columns].bitcast(FP8X4),
+                scales=scales[name][:, columns],
+                in_=grouped[name][:, columns, :].rearrange("p j i -> p (j i)"),
+            )
+
+        banks = {}
+
+        def open_bank(n, h):
+            banks[n, h] = psum.tile([P, BANK_TILES, CHUNK], F32, name="bank")
+            for s in range(BANK_TILES):
+                t = BANK_TILES * h + s
+                for a in range(0, CHUNK, W4_PASS):
+                    places = slice(n * CHUNK + a, n * CHUNK + a + W4_PASS)
                     nc.tensor.matmul_mx(
-                        out=acc[:, s, cols],
+                        out=banks[n, h][:, s, a : a + W4_PASS],
                         lhsT=w4_codes[:, 2 * P * t : 2 * P * (t + 1)].bitcast(FP4X4),
                         lhsT_scale=w4_plane[:, P * t : P * (t + 1)],
-                        rhs=x_codes[n][:, cols].bitcast(FP8X4),
-                        rhs_scale=x_scales[n][:, cols],
-                        start=True,
+                        rhs=codes["x"][:, places].bitcast(FP8X4),
+                        rhs_scale=scales["x"][:, places],
+                        start=(s == 0 and a == 0),
                         stop=False,
                     )
-                    nc.tensor.matmul_mx(
-                        out=acc[:, s, cols],
-                        lhsT=u_codes[h][:, P * s : P * (s + 1)].bitcast(FP8X4),
-                        lhsT_scale=u_scales[h][:, P * s : P * (s + 1)],
-                        rhs=c_codes[n][:, cols].bitcast(FP8X4),
-                        rhs_scale=c_scales[n][:, cols],
-                        start=False,
-                        stop=True,
+
+        def close_bank(n, h, tiles_a_store=BANK_TILES):
+            for s in range(BANK_TILES):
+                t = BANK_TILES * h + s
+                nc.tensor.matmul_mx(
+                    out=banks[n, h][:, s, :],
+                    lhsT=codes["u"][:, P * t : P * (t + 1)].bitcast(FP8X4),
+                    lhsT_scale=scales["u"][:, P * t : P * (t + 1)],
+                    rhs=codes["c"][:, chunk[n]].bitcast(FP8X4),
+                    rhs_scale=scales["c"][:, chunk[n]],
+                    start=False,
+                    stop=(s == BANK_TILES - 1),
+                )
+            for first in range(0, BANK_TILES, tiles_a_store):
+                t0 = BANK_TILES * h + first
+                result = keep.tile([P, tiles_a_store, CHUNK], F32, name=f"result{n}_{t0}")
+                for s in range(tiles_a_store):
+                    nc.scalar.activation(
+                        out=result[:, s, :], in_=banks[n, h][:, first + s, :], func=SILU, bias=bias[:, t0 + s : t0 + s + 1]
                     )
-            for s in range(2):
-                t = 2 * h + s
-                nc.scalar.activation(out=res[:, s, :], in_=acc[:, s, :], func=SILU, bias=bias[:, t : t + 1])
-            nc.sync.dma_start(out_rows[:, 2 * h : 2 * h + 2, starts[n] : starts[n] + w], res[:])
+                nc.sync.dma_start(out_rows[:, t0 : t0 + tiles_a_store, chunk[n]], result[:])
 
-        for i in range(3):
+        for i in range(2):
+            for places in halves:
+                gather(i, places)
+        for places in halves:
+            group_pair(on_scalar, 0, places)
+        for places in halves:
+            gather(2, places)
+
+        for n in range(2):
+            gather(3, chunk[n])
+        for n in range(2):
+            group_pair(on_vector, 1, chunk[n])
+        group(on_scalar, "c", c_raw[0], chunk[0])
+        group(on_scalar, "u", u_raw[0], chunk[0])
+        for n in range(2):
+            quantize("x", chunk[n])
+        for h in range(2):
+            open_bank(0, h)
+        gather(3, chunk[2])
+        quantize("c", chunk[0])
+        gather(3, chunk[3])
+        quantize("u", chunk[0])
+        group_pair(on_scalar, 1, chunk[2])
+        group(on_scalar, "u", u_raw[1], chunk[1])
+        group_pair(on_scalar, 1, chunk[3])
+        close_bank(0, 0)
+        for h in range(2):
+            open_bank(1, h)
+        quantize("u", chunk[1])
+        close_bank(0, 1)
+
+        for n in range(1, CHUNKS - 1):
+            group(on_vector, "c", c_raw[n], chunk[n])
+            quantize("x", chunk[n + 1])
+            quantize("c", chunk[n])
             for h in range(2):
-                gather(i, h * HALF, HALF)
-            if i == 1:
-                for n in range(len(CHUNKS)):
-                    pair_to_grouped(0, n, False)
+                close_bank(n, h)
+            for h in range(2):
+                open_bank(n + 1, h)
 
-        for n, w in enumerate(CHUNKS):
-            gather(3, starts[n], w)
-            pair_to_grouped(1, n, P23_ON_VECTOR[n])
-            if n == 0:
-                interleave(U_ON_VECTOR[0], u_grouped[0][:], u_raw[0][:])
-                quantize(u_codes[0][:], u_scales[0][:], u_grouped[0][:])
-            interleave(C_ON_VECTOR[n], c_grouped[n][:], c_raw[n][:])
-            quantize(x_codes[n][:], x_scales[n][:], x_grouped[n][:])
-            quantize(c_codes[n][:], c_scales[n][:], c_grouped[n][:])
-            multiply(n, 0)
-            if n == 0:
-                interleave(U_ON_VECTOR[1], u_grouped[1][:], u_raw[1][:])
-                quantize(u_codes[1][:], u_scales[1][:], u_grouped[1][:])
-            multiply(n, 1)
+        last = CHUNKS - 1
+        group(on_vector, "c", c_raw[last], chunk[last])
+        quantize("c", chunk[last])
+        close_bank(last, 0)
+        close_bank(last, 1, tiles_a_store=1)

@@ -27,6 +27,8 @@ CHUNKS = S // CHUNK
 W4_PASS = 128
 BANK_TILES = 2
 BANKS = 8
+LISTS = P // LIST_GROUP
+WGT_ROWS = LISTS * S // P
 
 
 def tile_list_hmix_silu_kernel(tc, xT, w4_words, w4_scales, c, u, wgt, b, offs, out):
@@ -44,6 +46,8 @@ def tile_list_hmix_silu_kernel(tc, xT, w4_words, w4_scales, c, u, wgt, b, offs, 
         keep = ctx.enter_context(tc.tile_pool(name="keep", bufs=1))
         psum = ctx.enter_context(tc.psum_pool(name="psum", bufs=BANKS))
 
+        small_rows = keep.tile([P, P], F32, name="small_rows")
+        nc.sync.dma_start(small_rows[0:WGT_ROWS, :], wgt.rearrange("(g r) (a n) -> r g a n", r=LIST_GROUP, n=P)[0])
         offsets = keep.tile([P, S // LIST_GROUP], U16, name="offsets")
         nc.sync.dma_start(offsets[:], offs)
 
@@ -52,10 +56,11 @@ def tile_list_hmix_silu_kernel(tc, xT, w4_words, w4_scales, c, u, wgt, b, offs, 
         nc.vector.memset(warm_in[:], 0.0)
         nc.scalar.activation(out=warm_out[:], in_=warm_in[:], func=SILU)
 
-        identity = keep.tile([P, P], F32, name="identity")
-        make_identity(nc, identity[:])
+        nc.gpsimd.memset(small_rows[WGT_ROWS:P, :], 0.0)
         bias_rows = keep.tile([P, P], F32, name="bias_rows")
         nc.vector.memset(bias_rows[:], 0.0)
+        identity = keep.tile([P, P], F32, name="identity")
+        make_identity(nc, identity[:])
         w4_plane = keep.tile([P, M], U8, name="w4_plane", align_bytes=64)
         nc.vector.memset(w4_plane[:].bitcast(I32), 0)
 
@@ -75,9 +80,7 @@ def tile_list_hmix_silu_kernel(tc, xT, w4_words, w4_scales, c, u, wgt, b, offs, 
         codes = {v: keep.tile([P, w], U32, name=f"{v}_codes", align_bytes=64) for v, w in widths.items()}
         scales = {v: keep.tile([P, w], U8, name=f"{v}_scales", align_bytes=64) for v, w in widths.items()}
 
-        nc.sync.dma_start(weights[:, halves[0]], wgt[:, halves[0]])
         nc.sync.dma_start(windows[0][:], x_rows[:, 0, :])
-        nc.sync.dma_start(weights[:, halves[1]], wgt[:, halves[1]])
         nc.sync.dma_start(windows[1][:], x_rows[:, 1, :])
         nc.sync.dma_start(windows[2][:], x_rows[:, 2, :])
         nc.scalar.dma_start(bias_rows[0:ROW_TILES, :], b.rearrange("(t p) -> t p", p=P))
@@ -94,10 +97,23 @@ def tile_list_hmix_silu_kernel(tc, xT, w4_words, w4_scales, c, u, wgt, b, offs, 
         for n in range(1, CHUNKS):
             nc.sync.dma_start(c_raw[n], c_rows[:, :, chunk[n]])
 
-        bias_bank = psum.tile([P, P], F32, name="bank")
-        nc.tensor.transpose(bias_bank[:], bias_rows[:], identity[:])
+        turned = psum.tile([P, P], F32, name="bank")
+        nc.tensor.transpose(turned[:], small_rows[:], identity[:])
+        by_block = turned[:, 0:WGT_ROWS].rearrange("n (g a) -> n a g", g=LISTS)
+        blocks = CHUNK // P
+        repeated = [keep.tile([P, blocks, LISTS, LIST_GROUP], F32, name=f"repeated{n}") for n in range(CHUNKS)]
+        for n in range(CHUNKS):
+            part = slice(blocks * n, blocks * (n + 1))
+            on_vector(out=repeated[n][:], in_=by_block[:, part, :].unsqueeze(3).to_broadcast([P, blocks, LISTS, LIST_GROUP]))
+        for n in range(CHUNKS):
+            spread = psum.tile([P, blocks + 1, P], F32, name="bank")
+            for a in range(blocks):
+                nc.tensor.transpose(spread[:, a, :], repeated[n][:, a, :, :].rearrange("n g r -> n (g r)"), identity[:])
+            on_scalar(out=weights[:, chunk[n]], in_=spread[:, 0:blocks, :].rearrange("p a n -> p (a n)"))
+
+        nc.tensor.transpose(spread[:, blocks, :], bias_rows[:], identity[:])
         bias = keep.tile([P, ROW_TILES], F32, name="bias")
-        nc.scalar.copy(out=bias[:], in_=bias_bank[:, 0:ROW_TILES])
+        nc.scalar.copy(out=bias[:], in_=spread[:, blocks, 0:ROW_TILES])
 
         def gather(i, places):
             nc.vector.tensor_tensor(
@@ -162,13 +178,13 @@ def tile_list_hmix_silu_kernel(tc, xT, w4_words, w4_scales, c, u, wgt, b, offs, 
                     )
                 nc.sync.dma_start(out_rows[:, t0 : t0 + tiles_a_store, chunk[n]], result[:])
 
-        for i in range(2):
-            for places in halves:
-                gather(i, places)
+        for places in chunk:
+            gather(0, places)
+        for places in halves:
+            gather(1, places)
         for places in halves:
             group_pair(on_scalar, 0, places)
-        for places in halves:
-            gather(2, places)
+        gather(2, slice(0, S))
 
         for n in range(2):
             gather(3, chunk[n])

@@ -71,49 +71,50 @@ def tile_list_hmix_silu_kernel(tc, xT, w4_words, w4_scales, c, u, wgt, b, offs, 
         first_pair = keep.tile([P, 2, S], F32, name="first_pair")
         stage = keep.tile([P, 1 + PLANES, S], F32, name="stage")
         picked = [first_pair[:], stage[:, 0:2, :]]
-        own = [keep.tile([P, PLANES, CHUNK], F32, name=f"raw{r}") for r in range(CHUNKS)]
-        c_raw = [stage[:, 1:, chunk[2]]] + [r[:] for r in own[1:]]
-        u_raw = [stage[:, 1:, chunk[3]], own[0][:]]
+        c_raw = [keep.tile([P, PLANES, CHUNK], F32, name=f"c_raw{n}") for n in range(CHUNKS)]
+        u_raw = [stage[:, 1:, chunk[2]], stage[:, 1:, chunk[3]]]
 
         widths = {"x": S, "c": S, "u": M}
-        grouped = {v: keep.tile([P, w, PLANES], BF16, name=f"{v}_grouped", align_bytes=64) for v, w in widths.items()}
-        codes = {v: keep.tile([P, w], U32, name=f"{v}_codes", align_bytes=64) for v, w in widths.items()}
+        x_grouped = keep.tile([P, S, PLANES], BF16, name="x_grouped", align_bytes=64)
+        grouped = {("x", n, 0): x_grouped[:, chunk[n], :] for n in range(CHUNKS)}
         scales = {v: keep.tile([P, w], U8, name=f"{v}_scales", align_bytes=64) for v, w in widths.items()}
+        codes = {}
 
-        nc.sync.dma_start(windows[0][:], x_rows[:, 0, :])
-        nc.sync.dma_start(windows[1][:], x_rows[:, 1, :])
-        nc.sync.dma_start(windows[2][:], x_rows[:, 2, :])
+        for i in range(3):
+            nc.sync.dma_start(windows[i][:], x_rows[:, i, :])
         nc.scalar.dma_start(bias_rows[0:ROW_TILES, :], b.rearrange("(t p) -> t p", p=P))
         for q in range(P // QUADRANT):
             nc.scalar.dma_start(
                 w4_plane[QUADRANT * q : QUADRANT * q + 4, :].bitcast(I32),
                 w4_scales[0][4 * q : 4 * q + 4, :].bitcast(I32),
             )
-        nc.sync.dma_start(windows[3][:], x_rows[:, 3, :])
         nc.sync.dma_start(w4_codes[:].bitcast(I32), w4_words[0].bitcast(I32))
-        nc.sync.dma_start(c_raw[0], c_rows[:, :, chunk[0]])
+        nc.sync.dma_start(windows[3][:], x_rows[:, 3, :])
+        nc.sync.dma_start(c_raw[0][:], c_rows[:, :, chunk[0]])
         for h in range(2):
             nc.sync.dma_start(u_raw[h], u_rows[:, :, chunk[h]])
         for n in range(1, CHUNKS):
-            nc.sync.dma_start(c_raw[n], c_rows[:, :, chunk[n]])
+            nc.sync.dma_start(c_raw[n][:], c_rows[:, :, chunk[n]])
 
         turned = psum.tile([P, P], F32, name="bank")
         nc.tensor.transpose(turned[:], small_rows[:], identity[:])
         by_block = turned[:, 0:WGT_ROWS].rearrange("n (g a) -> n a g", g=LISTS)
-        blocks = CHUNK // P
-        repeated = [keep.tile([P, blocks, LISTS, LIST_GROUP], F32, name=f"repeated{n}") for n in range(CHUNKS)]
-        for n in range(CHUNKS):
-            part = slice(blocks * n, blocks * (n + 1))
-            on_vector(out=repeated[n][:], in_=by_block[:, part, :].unsqueeze(3).to_broadcast([P, blocks, LISTS, LIST_GROUP]))
-        for n in range(CHUNKS):
-            spread = psum.tile([P, blocks + 1, P], F32, name="bank")
-            for a in range(blocks):
-                nc.tensor.transpose(spread[:, a, :], repeated[n][:, a, :, :].rearrange("n g r -> n (g r)"), identity[:])
-            on_scalar(out=weights[:, chunk[n]], in_=spread[:, 0:blocks, :].rearrange("p a n -> p (a n)"))
+        pieces = [slice(0, 1), slice(4, 6), slice(6, 8), slice(1, 4)]
+        repeated = []
+        for part in pieces:
+            count = part.stop - part.start
+            repeated.append(keep.tile([P, count, LISTS, LIST_GROUP], F32, name=f"repeated{part.start}"))
+            on_vector(out=repeated[-1][:], in_=by_block[:, part, :].unsqueeze(3).to_broadcast([P, count, LISTS, LIST_GROUP]))
+        for part, source in zip(pieces, repeated):
+            count = part.stop - part.start
+            spread = psum.tile([P, count + 1, P], F32, name="bank")
+            for a in range(count):
+                nc.tensor.transpose(spread[:, a, :], source[:, a, :, :].rearrange("n g r -> n (g r)"), identity[:])
+            on_scalar(out=weights[:, P * part.start : P * part.stop], in_=spread[:, 0:count, :].rearrange("p a n -> p (a n)"))
 
-        nc.tensor.transpose(spread[:, blocks, :], bias_rows[:], identity[:])
+        nc.tensor.transpose(spread[:, count, :], bias_rows[:], identity[:])
         bias = keep.tile([P, ROW_TILES], F32, name="bias")
-        nc.scalar.copy(out=bias[:], in_=spread[:, blocks, 0:ROW_TILES])
+        nc.scalar.copy(out=bias[:], in_=spread[:, count, 0:ROW_TILES])
 
         def gather(i, places):
             nc.vector.tensor_tensor(
@@ -124,25 +125,28 @@ def tile_list_hmix_silu_kernel(tc, xT, w4_words, w4_scales, c, u, wgt, b, offs, 
             )
 
         def group_pair(copy, h, places):
-            copy(out=grouped["x"][:, places, 2 * h : 2 * h + 2], in_=picked[h][:, :, places].rearrange("p i j -> p j i"))
+            copy(out=x_grouped[:, places, 2 * h : 2 * h + 2], in_=picked[h][:, :, places].rearrange("p i j -> p j i"))
 
-        def group(copy, name, raw, columns):
+        def group(copy, name, n, raw, part=slice(0, CHUNK)):
+            label = f"{name}{n}_{part.start}"
+            grouped[name, n, part.start] = keep.tile([P, part.stop - part.start, PLANES], BF16, name=label, tag=label, align_bytes=64)[:]
             copy(
-                out=grouped[name][:, columns, :].rearrange("p (g e) i -> p g i e", e=4),
-                in_=raw.rearrange("p i (g e) -> p g i e", e=4),
+                out=grouped[name, n, part.start].rearrange("p (g e) i -> p g i e", e=4),
+                in_=raw[:, :, part].rearrange("p i (g e) -> p g i e", e=4),
             )
 
-        def quantize(name, columns):
+        def quantize(name, n, part=slice(0, CHUNK), tag=""):
+            if (name, n) not in codes:
+                codes[name, n] = keep.tile([P, CHUNK], U32, name=f"{name}_codes{n}", tag=tag, align_bytes=64)[:]
             nc.vector.quantize_mx(
-                out=codes[name][:, columns].bitcast(FP8X4),
-                scales=scales[name][:, columns],
-                in_=grouped[name][:, columns, :].rearrange("p j i -> p (j i)"),
+                out=codes[name, n][:, part].bitcast(FP8X4),
+                scales=scales[name][:, n * CHUNK + part.start : n * CHUNK + part.stop],
+                in_=grouped[name, n, part.start].rearrange("p j i -> p (j i)"),
             )
 
         banks = {}
 
-        def open_bank(n, h):
-            banks[n, h] = psum.tile([P, BANK_TILES, CHUNK], F32, name="bank")
+        def w4_passes(n, h, first):
             for s in range(BANK_TILES):
                 t = BANK_TILES * h + s
                 for a in range(0, CHUNK, W4_PASS):
@@ -151,24 +155,29 @@ def tile_list_hmix_silu_kernel(tc, xT, w4_words, w4_scales, c, u, wgt, b, offs, 
                         out=banks[n, h][:, s, a : a + W4_PASS],
                         lhsT=w4_codes[:, 2 * P * t : 2 * P * (t + 1)].bitcast(FP4X4),
                         lhsT_scale=w4_plane[:, P * t : P * (t + 1)],
-                        rhs=codes["x"][:, places].bitcast(FP8X4),
+                        rhs=codes["x", n][:, a : a + W4_PASS].bitcast(FP8X4),
                         rhs_scale=scales["x"][:, places],
-                        start=(s == 0 and a == 0),
-                        stop=False,
+                        start=first and s == 0 and a == 0,
+                        stop=not first and s == BANK_TILES - 1 and a == CHUNK - W4_PASS,
                     )
 
-        def close_bank(n, h, tiles_a_store=BANK_TILES):
+        def u_passes(n, h, first):
             for s in range(BANK_TILES):
                 t = BANK_TILES * h + s
                 nc.tensor.matmul_mx(
                     out=banks[n, h][:, s, :],
-                    lhsT=codes["u"][:, P * t : P * (t + 1)].bitcast(FP8X4),
+                    lhsT=codes["u", h][:, P * s : P * (s + 1)].bitcast(FP8X4),
                     lhsT_scale=scales["u"][:, P * t : P * (t + 1)],
-                    rhs=codes["c"][:, chunk[n]].bitcast(FP8X4),
+                    rhs=codes["c", n].bitcast(FP8X4),
                     rhs_scale=scales["c"][:, chunk[n]],
-                    start=False,
-                    stop=(s == BANK_TILES - 1),
+                    start=first and s == 0,
+                    stop=not first and s == BANK_TILES - 1,
                 )
+
+        def bank(n, h, order, tiles_a_store=BANK_TILES):
+            banks[n, h] = psum.tile([P, BANK_TILES, CHUNK], F32, name="bank")
+            order[0](n, h, True)
+            order[1](n, h, False)
             for first in range(0, BANK_TILES, tiles_a_store):
                 t0 = BANK_TILES * h + first
                 result = keep.tile([P, tiles_a_store, CHUNK], F32, name=f"result{n}_{t0}")
@@ -178,48 +187,32 @@ def tile_list_hmix_silu_kernel(tc, xT, w4_words, w4_scales, c, u, wgt, b, offs, 
                     )
                 nc.sync.dma_start(out_rows[:, t0 : t0 + tiles_a_store, chunk[n]], result[:])
 
-        for places in chunk:
-            gather(0, places)
-        for places in halves:
+        for part in pieces:
+            gather(0, slice(P * part.start, P * part.stop))
+        for places in reversed(halves):
             gather(1, places)
-        for places in halves:
+        for places in reversed(halves):
             group_pair(on_scalar, 0, places)
         gather(2, slice(0, S))
-
         for n in range(2):
             gather(3, chunk[n])
+        group(on_scalar, "c", 0, c_raw[0][:])
+        for h in range(2):
+            group(on_scalar, "u", h, u_raw[h])
         for n in range(2):
             group_pair(on_vector, 1, chunk[n])
-        group(on_scalar, "c", c_raw[0], chunk[0])
-        group(on_scalar, "u", u_raw[0], chunk[0])
-        for n in range(2):
-            quantize("x", chunk[n])
-        for h in range(2):
-            open_bank(0, h)
+        quantize("x", 0)
+        quantize("c", 0)
         gather(3, chunk[2])
-        quantize("c", chunk[0])
-        gather(3, chunk[3])
-        quantize("u", chunk[0])
         group_pair(on_scalar, 1, chunk[2])
-        group(on_scalar, "u", u_raw[1], chunk[1])
-        group_pair(on_scalar, 1, chunk[3])
-        close_bank(0, 0)
         for h in range(2):
-            open_bank(1, h)
-        quantize("u", chunk[1])
-        close_bank(0, 1)
-
-        for n in range(1, CHUNKS - 1):
-            group(on_vector, "c", c_raw[n], chunk[n])
-            quantize("x", chunk[n + 1])
-            quantize("c", chunk[n])
-            for h in range(2):
-                close_bank(n, h)
-            for h in range(2):
-                open_bank(n + 1, h)
-
-        last = CHUNKS - 1
-        group(on_vector, "c", c_raw[last], chunk[last])
-        quantize("c", chunk[last])
-        close_bank(last, 0)
-        close_bank(last, 1, tiles_a_store=1)
+            quantize("u", h)
+            bank(0, h, (w4_passes, u_passes))
+        gather(3, chunk[3])
+        group_pair(on_scalar, 1, chunk[3])
+        for n in range(1, CHUNKS):
+            group(on_vector, "c", n, c_raw[n][:])
+            quantize("x", n, tag="u1_0" if n == 1 else f"c{n - 1}_0")
+            quantize("c", n)
+            bank(n, 0, (w4_passes, u_passes))
+            bank(n, 1, (u_passes, w4_passes), tiles_a_store=1 if n == CHUNKS - 1 else BANK_TILES)

@@ -72,7 +72,8 @@ def tile_list_hmix_silu_kernel(tc, xT, w4_words, w4_scales, c, u, wgt, b, offs, 
         stage = keep.tile([P, 1 + PLANES, S], F32, name="stage")
         picked = [first_pair[:], stage[:, 0:2, :]]
         c_raw = [keep.tile([P, PLANES, CHUNK], F32, name=f"c_raw{n}") for n in range(CHUNKS)]
-        u_raw = [stage[:, 1:, chunk[2]], stage[:, 1:, chunk[3]]]
+        u_second = keep.tile([P, PLANES, CHUNK], F32, name="u_second")
+        u_raw = [stage[:, 1:, 5 * P : 7 * P], u_second[:]]
 
         widths = {"x": S, "c": S, "u": M}
         x_grouped = keep.tile([P, S, PLANES], BF16, name="x_grouped", align_bytes=64)
@@ -201,18 +202,21 @@ def tile_list_hmix_silu_kernel(tc, xT, w4_words, w4_scales, c, u, wgt, b, offs, 
             group(on_scalar, "u", h, u_raw[h])
         for n in range(2):
             group_pair(on_vector, 1, chunk[n])
-        quantize("x", 0)
+        for n in range(2):
+            quantize("x", n)
         quantize("c", 0)
         gather(3, chunk[2])
-        group_pair(on_scalar, 1, chunk[2])
-        for h in range(2):
-            quantize("u", h)
-            bank(0, h, (w4_passes, u_passes))
+        quantize("u", 0)
         gather(3, chunk[3])
-        group_pair(on_scalar, 1, chunk[3])
+        for n in (2, 3):
+            group_pair(on_scalar, 1, chunk[n])
+        bank(0, 0, (w4_passes, u_passes))
+        quantize("u", 1)
+        bank(0, 1, (w4_passes, u_passes))
         for n in range(1, CHUNKS):
             group(on_vector, "c", n, c_raw[n][:])
-            quantize("x", n, tag="u1_0" if n == 1 else f"c{n - 1}_0")
+            if n < CHUNKS - 1:
+                quantize("x", n + 1, tag="u1_0" if n == 1 else "c1_0")
             quantize("c", n)
             bank(n, 0, (w4_passes, u_passes))
-            bank(n, 1, (u_passes, w4_passes), tiles_a_store=1 if n == CHUNKS - 1 else BANK_TILES)
+            bank(n, 1, (w4_passes, u_passes), tiles_a_store=1 if n == CHUNKS - 1 else BANK_TILES)

@@ -39,7 +39,6 @@ def tile_list_hmix_silu_kernel(tc, xT, w4_words, w4_scales, c, u, wgt, b, offs, 
 
     x_rows = xT.rearrange("(p i) t -> p i t", i=PLANES)
     c_rows = c.rearrange("(p i) j -> p i j", i=PLANES)
-    u_rows = u.rearrange("(p i) n -> p i n", i=PLANES)
     out_rows = out.rearrange("(t p) j -> p t j", p=P)
 
     with ExitStack() as ctx:
@@ -69,11 +68,11 @@ def tile_list_hmix_silu_kernel(tc, xT, w4_words, w4_scales, c, u, wgt, b, offs, 
         w4_codes = keep.tile([P, 2 * M], U8, name="w4_codes", align_bytes=64)
 
         first_pair = keep.tile([P, 2, S], F32, name="first_pair")
-        stage = keep.tile([P, 1 + PLANES, S], F32, name="stage")
-        picked = [first_pair[:], stage[:, 0:2, :]]
+        stage = keep.tile([P, 2 * S - CHUNK + PLANES * M], F32, name="stage")
+        picked = [first_pair[:], stage[:, 0 : 2 * S].rearrange("p (i j) -> p i j", i=2)]
         c_raw = [keep.tile([P, PLANES, CHUNK], F32, name=f"c_raw{n}") for n in range(CHUNKS)]
-        u_second = keep.tile([P, PLANES, CHUNK], F32, name="u_second")
-        u_raw = [stage[:, 1:, 5 * P : 7 * P], u_second[:]]
+        u_whole = stage[:, 2 * S - CHUNK :]
+        u_raw = [u_whole.rearrange("p (i n) -> p i n", i=PLANES)[:, :, chunk[h]] for h in range(2)]
 
         widths = {"x": S, "c": S, "u": M}
         x_grouped = keep.tile([P, S, PLANES], BF16, name="x_grouped", align_bytes=64)
@@ -92,15 +91,14 @@ def tile_list_hmix_silu_kernel(tc, xT, w4_words, w4_scales, c, u, wgt, b, offs, 
         nc.sync.dma_start(w4_codes[:].bitcast(I32), w4_words[0].bitcast(I32))
         nc.sync.dma_start(windows[3][:], x_rows[:, 3, :])
         nc.sync.dma_start(c_raw[0][:], c_rows[:, :, chunk[0]])
-        for h in range(2):
-            nc.sync.dma_start(u_raw[h], u_rows[:, :, chunk[h]])
+        nc.sync.dma_start(u_whole, u.rearrange("(p i) n -> p (i n)", i=PLANES))
         for n in range(1, CHUNKS):
             nc.sync.dma_start(c_raw[n][:], c_rows[:, :, chunk[n]])
 
         turned = psum.tile([P, P], F32, name="bank")
         nc.tensor.transpose(turned[:], small_rows[:], identity[:])
         by_block = turned[:, 0:WGT_ROWS].rearrange("n (g a) -> n a g", g=LISTS)
-        pieces = [slice(0, 1), slice(4, 6), slice(6, 8), slice(1, 4)]
+        pieces = [slice(0, 1), slice(1, 3), slice(6, 8), slice(3, 6)]
         repeated = []
         for part in pieces:
             count = part.stop - part.start
@@ -197,19 +195,18 @@ def tile_list_hmix_silu_kernel(tc, xT, w4_words, w4_scales, c, u, wgt, b, offs, 
         gather(2, slice(0, S))
         for n in range(2):
             gather(3, chunk[n])
-        group(on_scalar, "c", 0, c_raw[0][:])
-        for h in range(2):
-            group(on_scalar, "u", h, u_raw[h])
-        for n in range(2):
-            group_pair(on_vector, 1, chunk[n])
+        group(on_vector, "c", 0, c_raw[0][:])
+        gather(3, chunk[2])
+        for n in range(3):
+            group_pair(on_scalar, 1, chunk[n])
+        quantize("c", 0)
         for n in range(2):
             quantize("x", n)
-        quantize("c", 0)
-        gather(3, chunk[2])
+        group(on_vector, "u", 0, u_raw[0])
+        group(on_scalar, "u", 1, u_raw[1])
         quantize("u", 0)
         gather(3, chunk[3])
-        for n in (2, 3):
-            group_pair(on_scalar, 1, chunk[n])
+        group_pair(on_scalar, 1, chunk[3])
         bank(0, 0, (w4_passes, u_passes))
         quantize("u", 1)
         bank(0, 1, (w4_passes, u_passes))

@@ -46,7 +46,7 @@ def tile_list_hmix_silu_kernel(tc, xT, w4_words, w4_scales, c, u, wgt, b, offs, 
         psum = ctx.enter_context(tc.psum_pool(name="psum", bufs=BANKS))
 
         small_rows = keep.tile([P, P], F32, name="small_rows")
-        nc.sync.dma_start(small_rows[0:WGT_ROWS, :], wgt.rearrange("(g r) (a n) -> r g a n", r=LIST_GROUP, n=P)[0])
+        nc.scalar.dma_start(small_rows[0:WGT_ROWS, :], wgt.rearrange("(g r) (a n) -> r g a n", r=LIST_GROUP, n=P)[0])
         offsets = keep.tile([P, S // LIST_GROUP], U16, name="offsets")
         nc.sync.dma_start(offsets[:], offs)
 
@@ -63,15 +63,22 @@ def tile_list_hmix_silu_kernel(tc, xT, w4_words, w4_scales, c, u, wgt, b, offs, 
         w4_plane = keep.tile([P, M], U8, name="w4_plane", align_bytes=64)
         nc.vector.memset(w4_plane[:].bitcast(I32), 0)
 
-        weights = keep.tile([P, S], F32, name="weights")
         windows = [keep.tile([P, T], F32, name=f"window{i}") for i in range(PLANES)]
         w4_codes = keep.tile([P, 2 * M], U8, name="w4_codes", align_bytes=64)
 
         first_pair = keep.tile([P, 2, S], F32, name="first_pair")
-        stage = keep.tile([P, 2 * S - CHUNK + PLANES * M], F32, name="stage")
-        picked = [first_pair[:], stage[:, 0 : 2 * S].rearrange("p (i j) -> p i j", i=2)]
+        second_pair = keep.tile([P, 2, S - CHUNK], F32, name="second_pair")
+        stage = keep.tile([P, S + PLANES * M], F32, name="stage")
+        weights = stage[:, 0:S]
+        last_pair = stage[:, 0 : 2 * S].rearrange("p (i j) -> p i j", i=2)[:, :, 0:CHUNK]
+
+        def picked(h, places):
+            if h == 1 and places == chunk[-1]:
+                return last_pair
+            return (first_pair, second_pair)[h][:, :, places]
+
         c_raw = [keep.tile([P, PLANES, CHUNK], F32, name=f"c_raw{n}") for n in range(CHUNKS)]
-        u_whole = stage[:, 2 * S - CHUNK :]
+        u_whole = stage[:, S:]
         u_raw = [u_whole.rearrange("p (i n) -> p i n", i=PLANES)[:, :, chunk[h]] for h in range(2)]
 
         widths = {"x": S, "c": S, "u": M}
@@ -88,8 +95,8 @@ def tile_list_hmix_silu_kernel(tc, xT, w4_words, w4_scales, c, u, wgt, b, offs, 
                 w4_plane[QUADRANT * q : QUADRANT * q + 4, :].bitcast(I32),
                 w4_scales[0][4 * q : 4 * q + 4, :].bitcast(I32),
             )
-        nc.sync.dma_start(w4_codes[:].bitcast(I32), w4_words[0].bitcast(I32))
         nc.sync.dma_start(windows[3][:], x_rows[:, 3, :])
+        nc.sync.dma_start(w4_codes[:].bitcast(I32), w4_words[0].bitcast(I32))
         nc.sync.dma_start(c_raw[0][:], c_rows[:, :, chunk[0]])
         nc.sync.dma_start(u_whole, u.rearrange("(p i) n -> p (i n)", i=PLANES))
         for n in range(1, CHUNKS):
@@ -117,14 +124,14 @@ def tile_list_hmix_silu_kernel(tc, xT, w4_words, w4_scales, c, u, wgt, b, offs, 
 
         def gather(i, places):
             nc.vector.tensor_tensor(
-                picked[i // 2][:, i % 2, places],
+                picked(i // 2, places)[:, i % 2, :],
                 windows[i][:].indirect(offsets[:, places.start // LIST_GROUP : places.stop // LIST_GROUP]),
                 weights[:, places],
                 MULT,
             )
 
         def group_pair(copy, h, places):
-            copy(out=x_grouped[:, places, 2 * h : 2 * h + 2], in_=picked[h][:, :, places].rearrange("p i j -> p j i"))
+            copy(out=x_grouped[:, places, 2 * h : 2 * h + 2], in_=picked(h, places).rearrange("p i j -> p j i"))
 
         def group(copy, name, n, raw, part=slice(0, CHUNK)):
             label = f"{name}{n}_{part.start}"
@@ -192,18 +199,19 @@ def tile_list_hmix_silu_kernel(tc, xT, w4_words, w4_scales, c, u, wgt, b, offs, 
             gather(1, places)
         for places in reversed(halves):
             group_pair(on_scalar, 0, places)
-        gather(2, slice(0, S))
-        for n in range(2):
-            gather(3, chunk[n])
-        group(on_vector, "c", 0, c_raw[0][:])
-        gather(3, chunk[2])
+        gather(2, slice(0, S - CHUNK))
         for n in range(3):
-            group_pair(on_scalar, 1, chunk[n])
-        quantize("c", 0)
+            gather(3, chunk[n])
         for n in range(2):
-            quantize("x", n)
+            group_pair(on_scalar, 1, chunk[n])
+        group(on_scalar, "c", 0, c_raw[0][:])
+        quantize("x", 0)
+        group_pair(on_vector, 1, chunk[2])
+        quantize("x", 1)
+        gather(2, chunk[3])
         group(on_vector, "u", 0, u_raw[0])
         group(on_scalar, "u", 1, u_raw[1])
+        quantize("c", 0)
         quantize("u", 0)
         gather(3, chunk[3])
         group_pair(on_scalar, 1, chunk[3])
@@ -211,9 +219,13 @@ def tile_list_hmix_silu_kernel(tc, xT, w4_words, w4_scales, c, u, wgt, b, offs, 
         quantize("u", 1)
         bank(0, 1, (w4_passes, u_passes))
         for n in range(1, CHUNKS):
-            group(on_vector, "c", n, c_raw[n][:])
             if n < CHUNKS - 1:
+                group(on_vector, "c", n, c_raw[n][:])
                 quantize("x", n + 1, tag="u1_0" if n == 1 else "c1_0")
-            quantize("c", n)
+                quantize("c", n)
+            else:
+                for step in (lambda part: group(on_vector, "c", n, c_raw[n][:], part), lambda part: quantize("c", n, part)):
+                    for part in (slice(0, P), slice(P, CHUNK)):
+                        step(part)
             bank(n, 0, (w4_passes, u_passes))
             bank(n, 1, (w4_passes, u_passes), tiles_a_store=1 if n == CHUNKS - 1 else BANK_TILES)

@@ -67,18 +67,19 @@ def tile_list_hmix_silu_kernel(tc, xT, w4_words, w4_scales, c, u, wgt, b, offs, 
         w4_codes = keep.tile([P, 2 * M], U8, name="w4_codes", align_bytes=64)
 
         first_pair = keep.tile([P, 2, S], F32, name="first_pair")
-        second_pair = keep.tile([P, 2, S - CHUNK], F32, name="second_pair")
-        stage = keep.tile([P, S + PLANES * M], F32, name="stage")
-        weights = stage[:, 0:S]
-        last_pair = stage[:, 0 : 2 * S].rearrange("p (i j) -> p i j", i=2)[:, :, 0:CHUNK]
+        weights = keep.tile([P, S], F32, name="weights")
+        early = S - CHUNK
+        stage = keep.tile([P, 2 * early + P + PLANES * M], F32, name="stage")
+        second_pair = stage[:, 0 : 2 * early].rearrange("p (i j) -> p i j", i=2)
+        last_pair = stage[:, 0 : 4 * early].rearrange("p (i j) -> p i j", i=2)[:, :, 0:CHUNK]
 
         def picked(h, places):
-            if h == 1 and places == chunk[-1]:
-                return last_pair
+            if h == 1 and places.start >= S - CHUNK:
+                return last_pair[:, :, places.start - (S - CHUNK) : places.stop - (S - CHUNK)]
             return (first_pair, second_pair)[h][:, :, places]
 
         c_raw = [keep.tile([P, PLANES, CHUNK], F32, name=f"c_raw{n}") for n in range(CHUNKS)]
-        u_whole = stage[:, S:]
+        u_whole = stage[:, 2 * early + P :]
         u_raw = [u_whole.rearrange("p (i n) -> p i n", i=PLANES)[:, :, chunk[h]] for h in range(2)]
 
         widths = {"x": S, "c": S, "u": M}
@@ -208,12 +209,13 @@ def tile_list_hmix_silu_kernel(tc, xT, w4_words, w4_scales, c, u, wgt, b, offs, 
         quantize("x", 0)
         group_pair(on_vector, 1, chunk[2])
         quantize("x", 1)
+        gather(3, slice(S - CHUNK, S - P))
         gather(2, chunk[3])
         group(on_vector, "u", 0, u_raw[0])
         group(on_scalar, "u", 1, u_raw[1])
         quantize("c", 0)
         quantize("u", 0)
-        gather(3, chunk[3])
+        gather(3, slice(S - P, S))
         group_pair(on_scalar, 1, chunk[3])
         bank(0, 0, (w4_passes, u_passes))
         quantize("u", 1)
@@ -228,4 +230,4 @@ def tile_list_hmix_silu_kernel(tc, xT, w4_words, w4_scales, c, u, wgt, b, offs, 
                     for part in (slice(0, P), slice(P, CHUNK)):
                         step(part)
             bank(n, 0, (w4_passes, u_passes))
-            bank(n, 1, (w4_passes, u_passes), tiles_a_store=1 if n == CHUNKS - 1 else BANK_TILES)
+            bank(n, 1, (u_passes, w4_passes) if n == 1 else (w4_passes, u_passes), tiles_a_store=1 if n == CHUNKS - 1 else BANK_TILES)

@@ -98,9 +98,8 @@ def tile_list_hmix_silu_kernel(tc, xT, w4_words, w4_scales, c, u, wgt, b, offs, 
             )
         nc.sync.dma_start(windows[3][:], x_rows[:, 3, :])
         nc.sync.dma_start(w4_codes[:].bitcast(I32), w4_words[0].bitcast(I32))
-        nc.sync.dma_start(c_raw[0][:], c_rows[:, :, chunk[0]])
         nc.sync.dma_start(u_whole, u.rearrange("(p i) n -> p (i n)", i=PLANES))
-        for n in range(1, CHUNKS):
+        for n in range(CHUNKS):
             nc.sync.dma_start(c_raw[n][:], c_rows[:, :, chunk[n]])
 
         turned = psum.tile([P, P], F32, name="bank")
@@ -205,16 +204,16 @@ def tile_list_hmix_silu_kernel(tc, xT, w4_words, w4_scales, c, u, wgt, b, offs, 
             gather(3, chunk[n])
         for n in range(2):
             group_pair(on_scalar, 1, chunk[n])
-        group(on_scalar, "c", 0, c_raw[0][:])
+        for h in range(2):
+            group(on_scalar, "u", h, u_raw[h])
         quantize("x", 0)
         group_pair(on_vector, 1, chunk[2])
         quantize("x", 1)
         gather(3, slice(S - CHUNK, S - P))
         gather(2, chunk[3])
-        group(on_vector, "u", 0, u_raw[0])
-        group(on_scalar, "u", 1, u_raw[1])
-        quantize("c", 0)
+        group(on_vector, "c", 0, c_raw[0][:])
         quantize("u", 0)
+        quantize("c", 0)
         gather(3, slice(S - P, S))
         group_pair(on_scalar, 1, chunk[3])
         bank(0, 0, (w4_passes, u_passes))

@@ -212,9 +212,9 @@ def tile_list_hmix_silu_kernel(tc, xT, w4_words, w4_scales, c, u, wgt, b, offs, 
         gather(3, slice(S - CHUNK, S - P))
         gather(2, chunk[3])
         group(on_vector, "c", 0, c_raw[0][:])
+        gather(3, slice(S - P, S))
         quantize("u", 0)
         quantize("c", 0)
-        gather(3, slice(S - P, S))
         group_pair(on_scalar, 1, chunk[3])
         bank(0, 0, (w4_passes, u_passes))
         quantize("u", 1)
@@ -229,4 +229,4 @@ def tile_list_hmix_silu_kernel(tc, xT, w4_words, w4_scales, c, u, wgt, b, offs, 
                     for part in (slice(0, P), slice(P, CHUNK)):
                         step(part)
             bank(n, 0, (w4_passes, u_passes))
-            bank(n, 1, (u_passes, w4_passes) if n == 1 else (w4_passes, u_passes), tiles_a_store=1 if n == CHUNKS - 1 else BANK_TILES)
+            bank(n, 1, (w4_passes, u_passes), tiles_a_store=1 if n == CHUNKS - 1 else BANK_TILES)

@@ -133,11 +133,13 @@ def tile_list_hmix_silu_kernel(tc, xT, w4_words, w4_scales, c, u, wgt, b, offs, 
         def group_pair(copy, h, places):
             copy(out=x_grouped[:, places, 2 * h : 2 * h + 2], in_=picked(h, places).rearrange("p i j -> p j i"))
 
-        def group(copy, name, n, raw, part=slice(0, CHUNK)):
-            label = f"{name}{n}_{part.start}"
-            grouped[name, n, part.start] = keep.tile([P, part.stop - part.start, PLANES], BF16, name=label, tag=label, align_bytes=64)[:]
+        def group(copy, name, n, raw, part=slice(0, CHUNK), whole=None):
+            whole = whole or part
+            if (name, n, whole.start) not in grouped:
+                label = f"{name}{n}_{whole.start}"
+                grouped[name, n, whole.start] = keep.tile([P, whole.stop - whole.start, PLANES], BF16, name=label, tag=label, align_bytes=64)[:]
             copy(
-                out=grouped[name, n, part.start].rearrange("p (g e) i -> p g i e", e=4),
+                out=grouped[name, n, whole.start][:, part.start - whole.start : part.stop - whole.start, :].rearrange("p (g e) i -> p g i e", e=4),
                 in_=raw[:, :, part].rearrange("p i (g e) -> p g i e", e=4),
             )
 
@@ -204,15 +206,16 @@ def tile_list_hmix_silu_kernel(tc, xT, w4_words, w4_scales, c, u, wgt, b, offs, 
             gather(3, chunk[n])
         for n in range(2):
             group_pair(on_scalar, 1, chunk[n])
-        for h in range(2):
-            group(on_scalar, "u", h, u_raw[h])
+        for part in (slice(0, P), slice(P, CHUNK)):
+            group(on_scalar, "u", 0, u_raw[0], part, chunk[0])
+        group(on_scalar, "u", 1, u_raw[1])
         quantize("x", 0)
         group_pair(on_vector, 1, chunk[2])
         quantize("x", 1)
         gather(3, slice(S - CHUNK, S - P))
         gather(2, chunk[3])
-        group(on_vector, "c", 0, c_raw[0][:])
         gather(3, slice(S - P, S))
+        group(on_vector, "c", 0, c_raw[0][:])
         quantize("u", 0)
         quantize("c", 0)
         group_pair(on_scalar, 1, chunk[3])

@@ -68,18 +68,25 @@ def tile_list_hmix_silu_kernel(tc, xT, w4_words, w4_scales, c, u, wgt, b, offs, 
 
         first_pair = keep.tile([P, 2, S], F32, name="first_pair")
         weights = keep.tile([P, S], F32, name="weights")
-        early = S - CHUNK
-        stage = keep.tile([P, 2 * early + P + PLANES * M], F32, name="stage")
-        second_pair = stage[:, 0 : 2 * early].rearrange("p (i j) -> p i j", i=2)
-        last_pair = stage[:, 0 : 4 * early].rearrange("p (i j) -> p i j", i=2)[:, :, 0:CHUNK]
+        u_row = 11
+        stage = keep.tile([P, (u_row + 1) * P + PLANES * M], F32, name="stage")
+        row_of = {2: [0, 1, 2, 3, 4, 5, 0, 1], 3: [6, 7, 8, 9, u_row + PLANES * M // P, u_row + M // P, 10, u_row]}
 
-        def picked(h, places):
-            if h == 1 and places.start >= S - CHUNK:
-                return last_pair[:, :, places.start - (S - CHUNK) : places.stop - (S - CHUNK)]
-            return (first_pair, second_pair)[h][:, :, places]
+        def picked(i, places):
+            if i < 2:
+                return first_pair[:, i, places]
+            start = row_of[i][places.start // P] * P
+            return stage[:, start : start + places.stop - places.start]
+
+        def picked_pair(h, places):
+            if h == 0:
+                return first_pair[:, :, places]
+            width = places.stop - places.start
+            low, high = (row_of[i][places.start // P] * P // width for i in (2, 3))
+            return stage[:].rearrange("p (r j) -> p r j", j=width)[:, low : high + 1 : high - low, :]
 
         c_raw = [keep.tile([P, PLANES, CHUNK], F32, name=f"c_raw{n}") for n in range(CHUNKS)]
-        u_whole = stage[:, 2 * early + P :]
+        u_whole = stage[:, u_row * P : u_row * P + PLANES * M]
         u_raw = [u_whole.rearrange("p (i n) -> p i n", i=PLANES)[:, :, chunk[h]] for h in range(2)]
 
         widths = {"x": S, "c": S, "u": M}
@@ -124,14 +131,14 @@ def tile_list_hmix_silu_kernel(tc, xT, w4_words, w4_scales, c, u, wgt, b, offs, 
 
         def gather(i, places):
             nc.vector.tensor_tensor(
-                picked(i // 2, places)[:, i % 2, :],
+                picked(i, places),
                 windows[i][:].indirect(offsets[:, places.start // LIST_GROUP : places.stop // LIST_GROUP]),
                 weights[:, places],
                 MULT,
             )
 
         def group_pair(copy, h, places):
-            copy(out=x_grouped[:, places, 2 * h : 2 * h + 2], in_=picked(h, places).rearrange("p i j -> p j i"))
+            copy(out=x_grouped[:, places, 2 * h : 2 * h + 2], in_=picked_pair(h, places).rearrange("p i j -> p j i"))
 
         def group(copy, name, n, raw, part=slice(0, CHUNK), whole=None):
             whole = whole or part
@@ -152,46 +159,37 @@ def tile_list_hmix_silu_kernel(tc, xT, w4_words, w4_scales, c, u, wgt, b, offs, 
                 in_=grouped[name, n, part.start].rearrange("p j i -> p (j i)"),
             )
 
-        banks = {}
-
-        def w4_passes(n, h, first):
-            for s in range(BANK_TILES):
-                t = BANK_TILES * h + s
-                for a in range(0, CHUNK, W4_PASS):
-                    places = slice(n * CHUNK + a, n * CHUNK + a + W4_PASS)
-                    nc.tensor.matmul_mx(
-                        out=banks[n, h][:, s, a : a + W4_PASS],
-                        lhsT=w4_codes[:, 2 * P * t : 2 * P * (t + 1)].bitcast(FP4X4),
-                        lhsT_scale=w4_plane[:, P * t : P * (t + 1)],
-                        rhs=codes["x", n][:, a : a + W4_PASS].bitcast(FP8X4),
-                        rhs_scale=scales["x"][:, places],
-                        start=first and s == 0 and a == 0,
-                        stop=not first and s == BANK_TILES - 1 and a == CHUNK - W4_PASS,
-                    )
-
-        def u_passes(n, h, first):
-            for s in range(BANK_TILES):
-                t = BANK_TILES * h + s
+        def row_tile_sum(n, t):
+            sums = psum.tile([P, CHUNK], F32, name="bank")
+            for a in range(0, CHUNK, W4_PASS):
                 nc.tensor.matmul_mx(
-                    out=banks[n, h][:, s, :],
-                    lhsT=codes["u", h][:, P * s : P * (s + 1)].bitcast(FP8X4),
-                    lhsT_scale=scales["u"][:, P * t : P * (t + 1)],
-                    rhs=codes["c", n].bitcast(FP8X4),
-                    rhs_scale=scales["c"][:, chunk[n]],
-                    start=first and s == 0,
-                    stop=not first and s == BANK_TILES - 1,
+                    out=sums[:, a : a + W4_PASS],
+                    lhsT=w4_codes[:, 2 * P * t : 2 * P * (t + 1)].bitcast(FP4X4),
+                    lhsT_scale=w4_plane[:, P * t : P * (t + 1)],
+                    rhs=codes["x", n][:, a : a + W4_PASS].bitcast(FP8X4),
+                    rhs_scale=scales["x"][:, n * CHUNK + a : n * CHUNK + a + W4_PASS],
+                    start=a == 0,
+                    stop=False,
                 )
+            h, s = divmod(t, BANK_TILES)
+            nc.tensor.matmul_mx(
+                out=sums[:],
+                lhsT=codes["u", h][:, P * s : P * (s + 1)].bitcast(FP8X4),
+                lhsT_scale=scales["u"][:, P * t : P * (t + 1)],
+                rhs=codes["c", n].bitcast(FP8X4),
+                rhs_scale=scales["c"][:, chunk[n]],
+                start=False,
+                stop=True,
+            )
+            return sums
 
-        def bank(n, h, order, tiles_a_store=BANK_TILES):
-            banks[n, h] = psum.tile([P, BANK_TILES, CHUNK], F32, name="bank")
-            order[0](n, h, True)
-            order[1](n, h, False)
+        def bank(n, h, tiles_a_store=BANK_TILES):
             for first in range(0, BANK_TILES, tiles_a_store):
                 t0 = BANK_TILES * h + first
                 result = keep.tile([P, tiles_a_store, CHUNK], F32, name=f"result{n}_{t0}")
                 for s in range(tiles_a_store):
                     nc.scalar.activation(
-                        out=result[:, s, :], in_=banks[n, h][:, first + s, :], func=SILU, bias=bias[:, t0 + s : t0 + s + 1]
+                        out=result[:, s, :], in_=row_tile_sum(n, t0 + s)[:], func=SILU, bias=bias[:, t0 + s : t0 + s + 1]
                     )
                 nc.sync.dma_start(out_rows[:, t0 : t0 + tiles_a_store, chunk[n]], result[:])
 
@@ -201,35 +199,42 @@ def tile_list_hmix_silu_kernel(tc, xT, w4_words, w4_scales, c, u, wgt, b, offs, 
             gather(1, places)
         for places in reversed(halves):
             group_pair(on_scalar, 0, places)
+        block = [slice(a * P, (a + 1) * P) for a in range(S // P)]
         gather(2, slice(0, S - CHUNK))
-        for n in range(3):
+        for n in range(2):
             gather(3, chunk[n])
+        gather(3, block[4])
         for n in range(2):
             group_pair(on_scalar, 1, chunk[n])
         for part in (slice(0, P), slice(P, CHUNK)):
             group(on_scalar, "u", 0, u_raw[0], part, chunk[0])
         group(on_scalar, "u", 1, u_raw[1])
+        gather(3, block[6])
+        group_pair(on_vector, 1, block[4])
         quantize("x", 0)
-        group_pair(on_vector, 1, chunk[2])
-        quantize("x", 1)
-        gather(3, slice(S - CHUNK, S - P))
         gather(2, chunk[3])
-        gather(3, slice(S - P, S))
+        quantize("x", 1)
+        gather(3, block[5])
+        gather(3, block[7])
+        group_pair(on_scalar, 1, block[5])
+        group_pair(on_scalar, 1, chunk[3])
         group(on_vector, "c", 0, c_raw[0][:])
         quantize("u", 0)
         quantize("c", 0)
-        group_pair(on_scalar, 1, chunk[3])
-        bank(0, 0, (w4_passes, u_passes))
-        quantize("u", 1)
-        bank(0, 1, (w4_passes, u_passes))
-        for n in range(1, CHUNKS):
-            if n < CHUNKS - 1:
-                group(on_vector, "c", n, c_raw[n][:])
-                quantize("x", n + 1, tag="u1_0" if n == 1 else "c1_0")
-                quantize("c", n)
-            else:
-                for step in (lambda part: group(on_vector, "c", n, c_raw[n][:], part), lambda part: quantize("c", n, part)):
-                    for part in (slice(0, P), slice(P, CHUNK)):
-                        step(part)
-            bank(n, 0, (w4_passes, u_passes))
-            bank(n, 1, (w4_passes, u_passes), tiles_a_store=1 if n == CHUNKS - 1 else BANK_TILES)
+        bank(0, 0)
+        group(on_vector, "c", 1, c_raw[1][:])
+        quantize("u", 1, tag="c0_0")
+        bank(0, 1)
+        quantize("c", 1)
+        for h in range(2):
+            bank(1, h)
+        group(on_vector, "c", 2, c_raw[2][:])
+        quantize("x", 2, tag="c1_0")
+        quantize("c", 2)
+        for h in range(2):
+            bank(2, h)
+        group(on_vector, "c", 3, c_raw[3][:])
+        quantize("x", 3, tag="c2_0")
+        quantize("c", 3)
+        bank(3, 0)
+        bank(3, 1, tiles_a_store=1)

@@ -35,7 +35,8 @@ def tile_list_hmix_silu_kernel(tc, xT, w4_words, w4_scales, c, u, wgt, b, offs, 
     nc = tc.nc
     on_vector, on_scalar = nc.vector.tensor_copy, nc.scalar.copy
     chunk = [slice(n * CHUNK, (n + 1) * CHUNK) for n in range(CHUNKS)]
-    halves = [slice(0, S // 2), slice(S // 2, S)]
+    first_cut = 5 * P
+    halves = [slice(0, first_cut), slice(first_cut, S)]
 
     x_rows = xT.rearrange("(p i) t -> p i t", i=PLANES)
     c_rows = c.rearrange("(p i) j -> p i j", i=PLANES)
@@ -68,9 +69,9 @@ def tile_list_hmix_silu_kernel(tc, xT, w4_words, w4_scales, c, u, wgt, b, offs, 
 
         first_pair = keep.tile([P, 2, S], F32, name="first_pair")
         weights = keep.tile([P, S], F32, name="weights")
-        u_row = 11
-        stage = keep.tile([P, (u_row + 1) * P + PLANES * M], F32, name="stage")
-        row_of = {2: [0, 1, 2, 3, 4, 5, 0, 1], 3: [6, 7, 8, 9, u_row + PLANES * M // P, u_row + M // P, 10, u_row]}
+        u_row = 12
+        stage = keep.tile([P, u_row * P + PLANES * M], F32, name="stage")
+        row_of = {2: [0, 1, 2, 3, 4, 5, 0, 1], 3: [6, 7, 8, 9, 10, 11, 6, u_row]}
 
         def picked(i, places):
             if i < 2:
@@ -85,7 +86,7 @@ def tile_list_hmix_silu_kernel(tc, xT, w4_words, w4_scales, c, u, wgt, b, offs, 
             low, high = (row_of[i][places.start // P] * P // width for i in (2, 3))
             return stage[:].rearrange("p (r j) -> p r j", j=width)[:, low : high + 1 : high - low, :]
 
-        c_raw = [keep.tile([P, PLANES, CHUNK], F32, name=f"c_raw{n}") for n in range(CHUNKS)]
+        c_raw = [keep.tile([P, PLANES, CHUNK], F32, name=f"c_raw{n}", tag=f"c_raw{n}", align_bytes=64) for n in range(CHUNKS)]
         u_whole = stage[:, u_row * P : u_row * P + PLANES * M]
         u_raw = [u_whole.rearrange("p (i n) -> p i n", i=PLANES)[:, :, chunk[h]] for h in range(2)]
 
@@ -159,39 +160,39 @@ def tile_list_hmix_silu_kernel(tc, xT, w4_words, w4_scales, c, u, wgt, b, offs, 
                 in_=grouped[name, n, part.start].rearrange("p j i -> p (j i)"),
             )
 
-        def row_tile_sum(n, t):
-            sums = psum.tile([P, CHUNK], F32, name="bank")
-            for a in range(0, CHUNK, W4_PASS):
+        def bank(first, width, tiles, tiles_a_store):
+            n, start = divmod(first, CHUNK)
+            sums = psum.tile([P, len(tiles), width], F32, name="bank")
+            for s, t in enumerate(tiles):
+                for a in range(0, width, W4_PASS):
+                    nc.tensor.matmul_mx(
+                        out=sums[:, s, a : a + W4_PASS],
+                        lhsT=w4_codes[:, 2 * P * t : 2 * P * (t + 1)].bitcast(FP4X4),
+                        lhsT_scale=w4_plane[:, P * t : P * (t + 1)],
+                        rhs=codes["x", n][:, start + a : start + a + W4_PASS].bitcast(FP8X4),
+                        rhs_scale=scales["x"][:, first + a : first + a + W4_PASS],
+                        start=s == 0 and a == 0,
+                        stop=False,
+                    )
+            for s, t in enumerate(tiles):
+                h, column = divmod(P * t, CHUNK)
                 nc.tensor.matmul_mx(
-                    out=sums[:, a : a + W4_PASS],
-                    lhsT=w4_codes[:, 2 * P * t : 2 * P * (t + 1)].bitcast(FP4X4),
-                    lhsT_scale=w4_plane[:, P * t : P * (t + 1)],
-                    rhs=codes["x", n][:, a : a + W4_PASS].bitcast(FP8X4),
-                    rhs_scale=scales["x"][:, n * CHUNK + a : n * CHUNK + a + W4_PASS],
-                    start=a == 0,
-                    stop=False,
+                    out=sums[:, s, :],
+                    lhsT=codes["u", h][:, column : column + P].bitcast(FP8X4),
+                    lhsT_scale=scales["u"][:, P * t : P * (t + 1)],
+                    rhs=codes["c", n][:, start : start + width].bitcast(FP8X4),
+                    rhs_scale=scales["c"][:, first : first + width],
+                    start=False,
+                    stop=s == len(tiles) - 1,
                 )
-            h, s = divmod(t, BANK_TILES)
-            nc.tensor.matmul_mx(
-                out=sums[:],
-                lhsT=codes["u", h][:, P * s : P * (s + 1)].bitcast(FP8X4),
-                lhsT_scale=scales["u"][:, P * t : P * (t + 1)],
-                rhs=codes["c", n].bitcast(FP8X4),
-                rhs_scale=scales["c"][:, chunk[n]],
-                start=False,
-                stop=True,
-            )
-            return sums
-
-        def bank(n, h, tiles_a_store=BANK_TILES):
-            for first in range(0, BANK_TILES, tiles_a_store):
-                t0 = BANK_TILES * h + first
-                result = keep.tile([P, tiles_a_store, CHUNK], F32, name=f"result{n}_{t0}")
+            for s0 in range(0, len(tiles), tiles_a_store):
+                t0 = tiles[s0]
+                result = keep.tile([P, tiles_a_store, width], F32, name=f"result{first}_{t0}")
                 for s in range(tiles_a_store):
                     nc.scalar.activation(
-                        out=result[:, s, :], in_=row_tile_sum(n, t0 + s)[:], func=SILU, bias=bias[:, t0 + s : t0 + s + 1]
+                        out=result[:, s, :], in_=sums[:, s0 + s, :], func=SILU, bias=bias[:, t0 + s : t0 + s + 1]
                     )
-                nc.sync.dma_start(out_rows[:, t0 : t0 + tiles_a_store, chunk[n]], result[:])
+                nc.sync.dma_start(out_rows[:, t0 : t0 + tiles_a_store, first : first + width], result[:])
 
         for part in pieces:
             gather(0, slice(P * part.start, P * part.stop))
@@ -201,40 +202,30 @@ def tile_list_hmix_silu_kernel(tc, xT, w4_words, w4_scales, c, u, wgt, b, offs, 
             group_pair(on_scalar, 0, places)
         block = [slice(a * P, (a + 1) * P) for a in range(S // P)]
         gather(2, slice(0, S - CHUNK))
-        for n in range(2):
-            gather(3, chunk[n])
-        gather(3, block[4])
-        for n in range(2):
-            group_pair(on_scalar, 1, chunk[n])
+        for places in (block[0], block[1], chunk[1], chunk[2]):
+            gather(3, places)
+            group_pair(on_scalar, 1, places)
         for part in (slice(0, P), slice(P, CHUNK)):
             group(on_scalar, "u", 0, u_raw[0], part, chunk[0])
         group(on_scalar, "u", 1, u_raw[1])
-        gather(3, block[6])
-        group_pair(on_vector, 1, block[4])
         quantize("x", 0)
         gather(2, chunk[3])
+        gather(3, block[6])
         quantize("x", 1)
-        gather(3, block[5])
+        group_pair(on_vector, 1, block[6])
         gather(3, block[7])
-        group_pair(on_scalar, 1, block[5])
-        group_pair(on_scalar, 1, chunk[3])
+        group_pair(on_scalar, 1, block[7])
         group(on_vector, "c", 0, c_raw[0][:])
         quantize("u", 0)
         quantize("c", 0)
-        bank(0, 0)
-        group(on_vector, "c", 1, c_raw[1][:])
-        quantize("u", 1, tag="c0_0")
-        bank(0, 1)
-        quantize("c", 1)
-        for h in range(2):
-            bank(1, h)
-        group(on_vector, "c", 2, c_raw[2][:])
-        quantize("x", 2, tag="c1_0")
-        quantize("c", 2)
-        for h in range(2):
-            bank(2, h)
-        group(on_vector, "c", 3, c_raw[3][:])
-        quantize("x", 3, tag="c2_0")
-        quantize("c", 3)
-        bank(3, 0)
-        bank(3, 1, tiles_a_store=1)
+        bank(0, CHUNK, (0, 1), BANK_TILES)
+        late = {1: (("u", 1, "c0_0"), ("x", 2, "c_raw1")), 2: (("x", 3, "c1_0"),), 3: ()}
+        for n in range(1, CHUNKS):
+            group(on_vector, "c", n, c_raw[n][:])
+            for name, part, tag in late[n]:
+                quantize(name, part, tag=tag)
+            if n == 1:
+                bank(0, CHUNK, (2, 3), BANK_TILES)
+            quantize("c", n)
+            bank(n * CHUNK, CHUNK, (0, 1), BANK_TILES)
+            bank(n * CHUNK, CHUNK, (2, 3), 1 if n == CHUNKS - 1 else BANK_TILES)

@@ -24,7 +24,7 @@ QUADRANT = 32
 ROW_TILES = M // P
 CHUNK = 256
 CHUNKS = S // CHUNK
-W4_PASS = 128
+W4_PASS = 256
 BANK_TILES = 2
 BANKS = 8
 LISTS = P // LIST_GROUP

@@ -219,7 +219,7 @@ def tile_list_hmix_silu_kernel(tc, xT, w4_words, w4_scales, c, u, wgt, b, offs, 
         quantize("u", 0)
         quantize("c", 0)
         bank(0, CHUNK, (0, 1), BANK_TILES)
-        late = {1: (("u", 1, "c0_0"), ("x", 2, "c_raw1")), 2: (("x", 3, "c1_0"),), 3: ()}
+        late = {1: (("u", 1, "c0_0"),), 2: (("x", 2, "c1_0"),), 3: (("x", 3, "c2_0"),)}
         for n in range(1, CHUNKS):
             group(on_vector, "c", n, c_raw[n][:])
             for name, part, tag in late[n]:

@@ -218,7 +218,7 @@ def tile_list_hmix_silu_kernel(tc, xT, w4_words, w4_scales, c, u, wgt, b, offs, 
         group(on_vector, "c", 0, c_raw[0][:])
         quantize("u", 0)
         quantize("c", 0)
-        bank(0, CHUNK, (0, 1), BANK_TILES)
+        bank(0, CHUNK, (0, 1), 1)
         late = {1: (("u", 1, "c0_0"),), 2: (("x", 2, "c1_0"),), 3: (("x", 3, "c2_0"),)}
         for n in range(1, CHUNKS):
             group(on_vector, "c", n, c_raw[n][:])

@@ -225,7 +225,7 @@ def tile_list_hmix_silu_kernel(tc, xT, w4_words, w4_scales, c, u, wgt, b, offs, 
             for name, part, tag in late[n]:
                 quantize(name, part, tag=tag)
             if n == 1:
-                bank(0, CHUNK, (2, 3), BANK_TILES)
+                bank(0, CHUNK, (2, 3), 1)
             quantize("c", n)
-            bank(n * CHUNK, CHUNK, (0, 1), BANK_TILES)
-            bank(n * CHUNK, CHUNK, (2, 3), 1 if n == CHUNKS - 1 else BANK_TILES)
+            bank(n * CHUNK, CHUNK, (0, 1), 1)
+            bank(n * CHUNK, CHUNK, (2, 3), 1)

@@ -147,8 +147,8 @@ def tile_list_hmix_silu_kernel(tc, xT, w4_words, w4_scales, c, u, wgt, b, offs, 
                 label = f"{name}{n}_{whole.start}"
                 grouped[name, n, whole.start] = keep.tile([P, whole.stop - whole.start, PLANES], BF16, name=label, tag=label, align_bytes=64)[:]
             copy(
-                out=grouped[name, n, whole.start][:, part.start - whole.start : part.stop - whole.start, :].rearrange("p (g e) i -> p g i e", e=4),
-                in_=raw[:, :, part].rearrange("p i (g e) -> p g i e", e=4),
+                out=grouped[name, n, whole.start][:, part.start - whole.start : part.stop - whole.start, :].rearrange("p (g e) i -> p g i e", e=2),
+                in_=raw[:, :, part].rearrange("p i (g e) -> p g i e", e=2),
             )
 
         def quantize(name, n, part=slice(0, CHUNK), tag=""):

@@ -218,14 +218,16 @@ def tile_list_hmix_silu_kernel(tc, xT, w4_words, w4_scales, c, u, wgt, b, offs, 
         group(on_vector, "c", 0, c_raw[0][:])
         quantize("u", 0)
         quantize("c", 0)
-        bank(0, CHUNK, (0, 1), 1)
+        bank(0, CHUNK, (0,), 1)
+        bank(0, CHUNK, (1,), 1)
         late = {1: (("u", 1, "c0_0"),), 2: (("x", 2, "c1_0"),), 3: (("x", 3, "c2_0"),)}
         for n in range(1, CHUNKS):
             group(on_vector, "c", n, c_raw[n][:])
             for name, part, tag in late[n]:
                 quantize(name, part, tag=tag)
             if n == 1:
-                bank(0, CHUNK, (2, 3), 1)
+                bank(0, CHUNK, (2,), 1)
+                bank(0, CHUNK, (3,), 1)
             quantize("c", n)
             bank(n * CHUNK, CHUNK, (0, 1), 1)
             bank(n * CHUNK, CHUNK, (2, 3), 1)

@@ -229,5 +229,5 @@ def tile_list_hmix_silu_kernel(tc, xT, w4_words, w4_scales, c, u, wgt, b, offs, 
                 bank(0, CHUNK, (2,), 1)
                 bank(0, CHUNK, (3,), 1)
             quantize("c", n)
-            bank(n * CHUNK, CHUNK, (0, 1), 1)
-            bank(n * CHUNK, CHUNK, (2, 3), 1)
+            for t in range(ROW_TILES):
+                bank(n * CHUNK, CHUNK, (t,), 1)

@@ -160,6 +160,13 @@ def tile_list_hmix_silu_kernel(tc, xT, w4_words, w4_scales, c, u, wgt, b, offs, 
                 in_=grouped[name, n, part.start].rearrange("p j i -> p (j i)"),
             )
 
+        alone = [slice(t, t + 1) for t in range(ROW_TILES)]
+        low, high = slice(0, 2), slice(2, 4)
+        next_store = [[low, low, high, high] for n in range(CHUNKS)]
+        next_store[0][0:2] = alone[0:2]
+        next_store[-1][2:4] = alone[2:4]
+        results = {}
+
         def bank(first, width, tiles, tiles_a_store):
             n, start = divmod(first, CHUNK)
             sums = psum.tile([P, len(tiles), width], F32, name="bank")
@@ -185,14 +192,14 @@ def tile_list_hmix_silu_kernel(tc, xT, w4_words, w4_scales, c, u, wgt, b, offs, 
                     start=False,
                     stop=s == len(tiles) - 1,
                 )
-            for s0 in range(0, len(tiles), tiles_a_store):
-                t0 = tiles[s0]
-                result = keep.tile([P, tiles_a_store, width], F32, name=f"result{first}_{t0}")
-                for s in range(tiles_a_store):
-                    nc.scalar.activation(
-                        out=result[:, s, :], in_=sums[:, s0 + s, :], func=SILU, bias=bias[:, t0 + s : t0 + s + 1]
-                    )
-                nc.sync.dma_start(out_rows[:, t0 : t0 + tiles_a_store, first : first + width], result[:])
+            t = tiles[0]
+            stored = next_store[n][t]
+            if t == stored.start:
+                results[n, t] = keep.tile([P, stored.stop - t, width], F32, name=f"result{first}_{t}")
+            result = results[n, stored.start]
+            nc.scalar.activation(out=result[:, t - stored.start, :], in_=sums[:, 0, :], func=SILU, bias=bias[:, t : t + 1])
+            if t == stored.stop - 1:
+                nc.sync.dma_start(out_rows[:, stored, first : first + width], result[:])
 
         for part in pieces:
             gather(0, slice(P * part.start, P * part.stop))

@@ -27,6 +27,7 @@ CHUNKS = S // CHUNK
 W4_PASS = 256
 BANK_TILES = 2
 BANKS = 8
+NARROW_TILES = 2
 LISTS = P // LIST_GROUP
 WGT_ROWS = LISTS * S // P
 
@@ -160,11 +161,6 @@ def tile_list_hmix_silu_kernel(tc, xT, w4_words, w4_scales, c, u, wgt, b, offs, 
                 in_=grouped[name, n, part.start].rearrange("p j i -> p (j i)"),
             )
 
-        alone = [slice(t, t + 1) for t in range(ROW_TILES)]
-        low, high = slice(0, 2), slice(2, 4)
-        next_store = [[low, low, high, high] for n in range(CHUNKS)]
-        next_store[0][0:2] = alone[0:2]
-        next_store[-1][2:4] = alone[2:4]
         results = {}
 
         def bank(first, width, tiles, tiles_a_store):
@@ -193,13 +189,16 @@ def tile_list_hmix_silu_kernel(tc, xT, w4_words, w4_scales, c, u, wgt, b, offs, 
                     stop=s == len(tiles) - 1,
                 )
             t = tiles[0]
-            stored = next_store[n][t]
-            if t == stored.start:
-                results[n, t] = keep.tile([P, stored.stop - t, width], F32, name=f"result{first}_{t}")
-            result = results[n, stored.start]
-            nc.scalar.activation(out=result[:, t - stored.start, :], in_=sums[:, 0, :], func=SILU, bias=bias[:, t : t + 1])
-            if t == stored.stop - 1:
-                nc.sync.dma_start(out_rows[:, stored, first : first + width], result[:])
+            wide = t >= NARROW_TILES
+            start_of = first - first % (2 * CHUNK) if wide else first
+            if (start_of, t) not in results:
+                results[start_of, t] = keep.tile([P, 2 * CHUNK if wide else CHUNK], F32, name=f"result{start_of}_{t}")
+            result = results[start_of, t]
+            nc.scalar.activation(
+                out=result[:, first - start_of : first - start_of + width], in_=sums[:, 0, :], func=SILU, bias=bias[:, t : t + 1]
+            )
+            if first + width == start_of + result.shape[1]:
+                nc.sync.dma_start(out_rows[:, t, start_of : first + width], result[:])
 
         for part in pieces:
             gather(0, slice(P * part.start, P * part.stop))
@@ -237,4 +236,4 @@ def tile_list_hmix_silu_kernel(tc, xT, w4_words, w4_scales, c, u, wgt, b, offs, 
                 bank(0, CHUNK, (3,), 1)
             quantize("c", n)
             for t in range(ROW_TILES):
-                bank(n * CHUNK, CHUNK, (t,), 1)
+                bank(n * CHUNK, CHUNK, ((t + NARROW_TILES * (n % 2)) % ROW_TILES,), 1)

@@ -27,7 +27,6 @@ CHUNKS = S // CHUNK
 W4_PASS = 256
 BANK_TILES = 2
 BANKS = 8
-NARROW_TILES = 2
 LISTS = P // LIST_GROUP
 WGT_ROWS = LISTS * S // P
 
@@ -161,6 +160,7 @@ def tile_list_hmix_silu_kernel(tc, xT, w4_words, w4_scales, c, u, wgt, b, offs, 
                 in_=grouped[name, n, part.start].rearrange("p j i -> p (j i)"),
             )
 
+        tile_order = [[(t - n) % ROW_TILES for t in range(ROW_TILES)] for n in range(CHUNKS)]
         results = {}
 
         def bank(first, width, tiles, tiles_a_store):
@@ -189,10 +189,11 @@ def tile_list_hmix_silu_kernel(tc, xT, w4_words, w4_scales, c, u, wgt, b, offs, 
                     stop=s == len(tiles) - 1,
                 )
             t = tiles[0]
-            wide = t >= NARROW_TILES
-            start_of = first - first % (2 * CHUNK) if wide else first
-            if (start_of, t) not in results:
-                results[start_of, t] = keep.tile([P, 2 * CHUNK if wide else CHUNK], F32, name=f"result{start_of}_{t}")
+            joins_last = n > 0 and t == tile_order[n][0]
+            waits = n < CHUNKS - 1 and t == tile_order[n][-1]
+            start_of = first - CHUNK if joins_last else first
+            if not joins_last:
+                results[start_of, t] = keep.tile([P, 2 * CHUNK if waits else CHUNK], F32, name=f"result{start_of}_{t}")
             result = results[start_of, t]
             nc.scalar.activation(
                 out=result[:, first - start_of : first - start_of + width], in_=sums[:, 0, :], func=SILU, bias=bias[:, t : t + 1]
@@ -235,5 +236,5 @@ def tile_list_hmix_silu_kernel(tc, xT, w4_words, w4_scales, c, u, wgt, b, offs, 
                 bank(0, CHUNK, (2,), 1)
                 bank(0, CHUNK, (3,), 1)
             quantize("c", n)
-            for t in range(ROW_TILES):
-                bank(n * CHUNK, CHUNK, ((t + NARROW_TILES * (n % 2)) % ROW_TILES,), 1)
+            for t in tile_order[n]:
+                bank(n * CHUNK, CHUNK, (t,), 1)

from contextlib import ExitStack

import concourse.mybir as mybir
from concourse.masks import make_identity

K, L, M, T, S = 512, 512, 512, 2048, 1024
FLOPS = 2 * (K + L) * M * S

F32 = mybir.dt.float32
BF16 = mybir.dt.bfloat16
I32 = mybir.dt.int32
U32 = mybir.dt.uint32
U16 = mybir.dt.uint16
U8 = mybir.dt.uint8
FP8X4 = mybir.dt.float8_e4m3fn_x4
FP4X4 = mybir.dt.float4_e2m1fn_x4
MULT = mybir.AluOpType.mult
SILU = mybir.ActivationFunctionType.Silu

P = 128
PLANES = 4
LIST_GROUP = 16
QUADRANT = 32
ROW_TILES = M // P
CHUNK = 256
CHUNKS = S // CHUNK
W4_PASS = 256
BANK_TILES = 2
BANKS = 8
LISTS = P // LIST_GROUP
WGT_ROWS = LISTS * S // P


def tile_list_hmix_silu_kernel(tc, xT, w4_words, w4_scales, c, u, wgt, b, offs, out):
    nc = tc.nc
    on_vector, on_scalar = nc.vector.tensor_copy, nc.scalar.copy
    chunk = [slice(n * CHUNK, (n + 1) * CHUNK) for n in range(CHUNKS)]
    first_cut = 5 * P
    halves = [slice(0, first_cut), slice(first_cut, S)]

    x_rows = xT.rearrange("(p i) t -> p i t", i=PLANES)
    c_rows = c.rearrange("(p i) j -> p i j", i=PLANES)
    out_rows = out.rearrange("(t p) j -> p t j", p=P)

    with ExitStack() as ctx:
        keep = ctx.enter_context(tc.tile_pool(name="keep", bufs=1))
        psum = ctx.enter_context(tc.psum_pool(name="psum", bufs=BANKS))

        small_rows = keep.tile([P, P], F32, name="small_rows")
        nc.scalar.dma_start(small_rows[0:WGT_ROWS, :], wgt.rearrange("(g r) (a n) -> r g a n", r=LIST_GROUP, n=P)[0])
        offsets = keep.tile([P, S // LIST_GROUP], U16, name="offsets")
        nc.sync.dma_start(offsets[:], offs)

        warm_in = keep.tile([P, 8], F32, name="warm_in")
        warm_out = keep.tile([P, 8], F32, name="warm_out")
        nc.vector.memset(warm_in[:], 0.0)
        nc.scalar.activation(out=warm_out[:], in_=warm_in[:], func=SILU)

        nc.gpsimd.memset(small_rows[WGT_ROWS:P, :], 0.0)
        bias_rows = keep.tile([P, P], F32, name="bias_rows")
        nc.vector.memset(bias_rows[:], 0.0)
        identity = keep.tile([P, P], F32, name="identity")
        make_identity(nc, identity[:])
        w4_plane = keep.tile([P, M], U8, name="w4_plane", align_bytes=64)
        nc.vector.memset(w4_plane[:].bitcast(I32), 0)

        windows = [keep.tile([P, T], F32, name=f"window{i}") for i in range(PLANES)]
        w4_codes = keep.tile([P, 2 * M], U8, name="w4_codes", align_bytes=64)

        first_pair = keep.tile([P, 2, S], F32, name="first_pair")
        weights = keep.tile([P, S], F32, name="weights")
        u_row = 12
        stage = keep.tile([P, u_row * P + PLANES * M], F32, name="stage")
        row_of = {2: [0, 1, 2, 3, 4, 5, 0, 1], 3: [6, 7, 8, 9, 10, 11, 6, u_row]}

        def picked(i, places):
            if i < 2:
                return first_pair[:, i, places]
            start = row_of[i][places.start // P] * P
            return stage[:, start : start + places.stop - places.start]

        def picked_pair(h, places):
            if h == 0:
                return first_pair[:, :, places]
            width = places.stop - places.start
            low, high = (row_of[i][places.start // P] * P // width for i in (2, 3))
            return stage[:].rearrange("p (r j) -> p r j", j=width)[:, low : high + 1 : high - low, :]

        c_raw = [keep.tile([P, PLANES, CHUNK], F32, name=f"c_raw{n}", tag=f"c_raw{n}", align_bytes=64) for n in range(CHUNKS)]
        u_whole = stage[:, u_row * P : u_row * P + PLANES * M]
        u_raw = [u_whole.rearrange("p (i n) -> p i n", i=PLANES)[:, :, chunk[h]] for h in range(2)]

        widths = {"x": S, "c": S, "u": M}
        x_grouped = keep.tile([P, S, PLANES], BF16, name="x_grouped", align_bytes=64)
        grouped = {("x", n, 0): x_grouped[:, chunk[n], :] for n in range(CHUNKS)}
        scales = {v: keep.tile([P, w], U8, name=f"{v}_scales", align_bytes=64) for v, w in widths.items()}
        codes = {}

        for i in range(3):
            nc.sync.dma_start(windows[i][:], x_rows[:, i, :])
        nc.scalar.dma_start(bias_rows[0:ROW_TILES, :], b.rearrange("(t p) -> t p", p=P))
        for q in range(P // QUADRANT):
            nc.scalar.dma_start(
                w4_plane[QUADRANT * q : QUADRANT * q + 4, :].bitcast(I32),
                w4_scales[0][4 * q : 4 * q + 4, :].bitcast(I32),
            )
        nc.sync.dma_start(windows[3][:], x_rows[:, 3, :])
        nc.sync.dma_start(w4_codes[:].bitcast(I32), w4_words[0].bitcast(I32))
        nc.sync.dma_start(u_whole, u.rearrange("(p i) n -> p (i n)", i=PLANES))
        for n in range(CHUNKS):
            nc.sync.dma_start(c_raw[n][:], c_rows[:, :, chunk[n]])

        turned = psum.tile([P, P], F32, name="bank")
        nc.tensor.transpose(turned[:], small_rows[:], identity[:])
        by_block = turned[:, 0:WGT_ROWS].rearrange("n (g a) -> n a g", g=LISTS)
        pieces = [slice(0, 1), slice(1, 3), slice(6, 8), slice(3, 6)]
        repeated = []
        for part in pieces:
            count = part.stop - part.start
            repeated.append(keep.tile([P, count, LISTS, LIST_GROUP], F32, name=f"repeated{part.start}"))
            on_vector(out=repeated[-1][:], in_=by_block[:, part, :].unsqueeze(3).to_broadcast([P, count, LISTS, LIST_GROUP]))
        for part, source in zip(pieces, repeated):
            count = part.stop - part.start
            spread = psum.tile([P, count + 1, P], F32, name="bank")
            for a in range(count):
                nc.tensor.transpose(spread[:, a, :], source[:, a, :, :].rearrange("n g r -> n (g r)"), identity[:])
            on_scalar(out=weights[:, P * part.start : P * part.stop], in_=spread[:, 0:count, :].rearrange("p a n -> p (a n)"))

        nc.tensor.transpose(spread[:, count, :], bias_rows[:], identity[:])
        bias = keep.tile([P, ROW_TILES], F32, name="bias")
        nc.scalar.copy(out=bias[:], in_=spread[:, count, 0:ROW_TILES])

        def gather(i, places):
            nc.vector.tensor_tensor(
                picked(i, places),
                windows[i][:].indirect(offsets[:, places.start // LIST_GROUP : places.stop // LIST_GROUP]),
                weights[:, places],
                MULT,
            )

        def group_pair(copy, h, places):
            copy(out=x_grouped[:, places, 2 * h : 2 * h + 2], in_=picked_pair(h, places).rearrange("p i j -> p j i"))

        def group(copy, name, n, raw, part=slice(0, CHUNK), whole=None):
            whole = whole or part
            if (name, n, whole.start) not in grouped:
                label = f"{name}{n}_{whole.start}"
                grouped[name, n, whole.start] = keep.tile([P, whole.stop - whole.start, PLANES], BF16, name=label, tag=label, align_bytes=64)[:]
            copy(
                out=grouped[name, n, whole.start][:, part.start - whole.start : part.stop - whole.start, :].rearrange("p (g e) i -> p g i e", e=2),
                in_=raw[:, :, part].rearrange("p i (g e) -> p g i e", e=2),
            )

        def quantize(name, n, part=slice(0, CHUNK), tag=""):
            if (name, n) not in codes:
                codes[name, n] = keep.tile([P, CHUNK], U32, name=f"{name}_codes{n}", tag=tag, align_bytes=64)[:]
            nc.vector.quantize_mx(
                out=codes[name, n][:, part].bitcast(FP8X4),
                scales=scales[name][:, n * CHUNK + part.start : n * CHUNK + part.stop],
                in_=grouped[name, n, part.start].rearrange("p j i -> p (j i)"),
            )

        tile_order = [[(t - n) % ROW_TILES for t in range(ROW_TILES)] for n in range(CHUNKS)]
        results = {}

        def bank(first, width, tiles, tiles_a_store):
            n, start = divmod(first, CHUNK)
            sums = psum.tile([P, len(tiles), width], F32, name="bank")
            for s, t in enumerate(tiles):
                for a in range(0, width, W4_PASS):
                    nc.tensor.matmul_mx(
                        out=sums[:, s, a : a + W4_PASS],
                        lhsT=w4_codes[:, 2 * P * t : 2 * P * (t + 1)].bitcast(FP4X4),
                        lhsT_scale=w4_plane[:, P * t : P * (t + 1)],
                        rhs=codes["x", n][:, start + a : start + a + W4_PASS].bitcast(FP8X4),
                        rhs_scale=scales["x"][:, first + a : first + a + W4_PASS],
                        start=s == 0 and a == 0,
                        stop=False,
                    )
            for s, t in enumerate(tiles):
                h, column = divmod(P * t, CHUNK)
                nc.tensor.matmul_mx(
                    out=sums[:, s, :],
                    lhsT=codes["u", h][:, column : column + P].bitcast(FP8X4),
                    lhsT_scale=scales["u"][:, P * t : P * (t + 1)],
                    rhs=codes["c", n][:, start : start + width].bitcast(FP8X4),
                    rhs_scale=scales["c"][:, first : first + width],
                    start=False,
                    stop=s == len(tiles) - 1,
                )
            t = tiles[0]
            joins_last = n > 0 and t == tile_order[n][0]
            waits = n < CHUNKS - 1 and t == tile_order[n][-1]
            start_of = first - CHUNK if joins_last else first
            if not joins_last:
                results[start_of, t] = keep.tile([P, 2 * CHUNK if waits else CHUNK], F32, name=f"result{start_of}_{t}")
            result = results[start_of, t]
            nc.scalar.activation(
                out=result[:, first - start_of : first - start_of + width], in_=sums[:, 0, :], func=SILU, bias=bias[:, t : t + 1]
            )
            if first + width == start_of + result.shape[1]:
                nc.sync.dma_start(out_rows[:, t, start_of : first + width], result[:])

        for part in pieces:
            gather(0, slice(P * part.start, P * part.stop))
        for places in reversed(halves):
            gather(1, places)
        for places in reversed(halves):
            group_pair(on_scalar, 0, places)
        block = [slice(a * P, (a + 1) * P) for a in range(S // P)]
        gather(2, slice(0, S - CHUNK))
        for places in (block[0], block[1], chunk[1], chunk[2]):
            gather(3, places)
            group_pair(on_scalar, 1, places)
        for part in (slice(0, P), slice(P, CHUNK)):
            group(on_scalar, "u", 0, u_raw[0], part, chunk[0])
        group(on_scalar, "u", 1, u_raw[1])
        quantize("x", 0)
        gather(2, chunk[3])
        gather(3, block[6])
        quantize("x", 1)
        group_pair(on_vector, 1, block[6])
        gather(3, block[7])
        group_pair(on_scalar, 1, block[7])
        group(on_vector, "c", 0, c_raw[0][:])
        quantize("u", 0)
        quantize("c", 0)
        bank(0, CHUNK, (0,), 1)
        bank(0, CHUNK, (1,), 1)
        late = {1: (("u", 1, "c0_0"),), 2: (("x", 2, "c1_0"),), 3: (("x", 3, "c2_0"),)}
        for n in range(1, CHUNKS):
            group(on_vector, "c", n, c_raw[n][:])
            for name, part, tag in late[n]:
                quantize(name, part, tag=tag)
            if n == 1:
                bank(0, CHUNK, (2,), 1)
                bank(0, CHUNK, (3,), 1)
            quantize("c", n)
            for t in tile_order[n]:
                bank(n * CHUNK, CHUNK, (t,), 1)
